import numpy as np
import ml_dtypes


def mxq(x, axis, fmt="e4m3"):
    dtype, down = {"e4m3": (ml_dtypes.float8_e4m3fn, 7), "e5m2": (ml_dtypes.float8_e5m2, 14)}[fmt]
    v = np.moveaxis(np.asarray(x, np.float32).astype(ml_dtypes.bfloat16).astype(np.float64), axis, -1)
    blocks = v.reshape(v.shape[:-1] + (-1, 32))
    amax = np.abs(blocks).max(-1, keepdims=True)
    byte = np.maximum(np.where(amax > 0, np.frexp(amax)[1] - 1 + 127, 0) - down, 1)
    scale = np.exp2(byte - 127.0)
    codes = (blocks / scale).astype(np.float32).astype(dtype).astype(np.float64)
    return np.moveaxis((codes * scale).reshape(v.shape), -1, axis)


WIDE = False


def mx_kscale(k):
    if not WIDE:
        return np.ones(k)
    levels = np.array([10, -10, 5, -5, 0])
    if k % 512:
        return np.exp2(np.random.permutation(np.resize(levels, k // 32))).repeat(32)
    a = np.empty((k // 512, 16))
    for p in range(k // 512):
        a[p, :8] = np.random.permutation(np.resize(levels, 8))
        for g in range(8):
            far = levels[np.abs(levels - a[p, g]) >= 10]
            a[p, g + 8] = far[np.random.randint(len(far))]
    return np.exp2(a.ravel()).repeat(32)


def f64(x):
    return np.asarray(x).astype(np.float64)


def striped(idx):
    return np.tile(idx.reshape(-1, 16).T, (8, 1)).astype(np.uint16)


def unstriped(offs):
    return offs[:16].T.reshape(-1).astype(np.int64)


E2M1 = np.array([0.0, 0.5, 1.0, 1.5, 2.0, 3.0, 4.0, 6.0, -0.0, -0.5, -1.0, -1.5, -2.0, -3.0, -4.0, -6.0])


def pack_weight(w, fmt):
    k, n = w.shape
    w = f64(np.asarray(w, np.float32).astype(ml_dtypes.bfloat16)).reshape(k // 32, 32, n)
    amax = np.abs(w).max(1)
    if fmt == "e4m3":
        byte = np.frexp(amax)[1] - 1 + 127 - 7
    else:
        mant, ex = np.frexp(amax / 6.0)
        byte = np.where(mant > 0.5, ex, ex - 1) + 127
    byte = np.clip(np.where(amax > 0, byte, 1), 1, 254)
    scaled = (w * np.exp2(127.0 - byte)[:, None, :]).reshape(k, n).astype(np.float32)
    by_word = np.ascontiguousarray(scaled.reshape(k // 512, 128, 4, n).transpose(0, 1, 3, 2))
    if fmt == "e4m3":
        words = by_word.astype(ml_dtypes.float8_e4m3fn).view(np.uint8)
    else:
        c = by_word.astype(ml_dtypes.float4_e2m1fn).view(np.uint8) & 0xF
        words = (c[..., 0::2] | (c[..., 1::2] << 4)).reshape(k // 512, 128, 2 * n)
    return np.ascontiguousarray(words), np.ascontiguousarray(byte.astype(np.uint8).reshape(k // 512, 16, n))


def unpack_weight(words, scales, fmt):
    g, _, n = scales.shape
    words = np.ascontiguousarray(words).reshape(g, 128, n, -1)
    if fmt == "e4m3":
        vals = words.view(ml_dtypes.float8_e4m3fn).astype(np.float64)
    else:
        nib = np.empty((g, 128, n, 4), np.uint8)
        nib[..., 0::2] = words & 0xF
        nib[..., 1::2] = words >> 4
        vals = E2M1[nib]
    vals = vals * np.repeat(np.exp2(scales.astype(np.float64) - 127.0), 8, axis=1)[..., None]
    return vals.transpose(0, 1, 3, 2).reshape(g * 512, n)


def gelu(v):
    return 0.5 * v * (1.0 + np.tanh(np.sqrt(2.0 / np.pi) * (v + 0.044715 * v**3)))


K, T, S, H, N = 1024, 4096, 1024, 512, 256

def setup_inputs():
    n = np.random.standard_normal
    s = mx_kscale(K)[:, None]
    u = mx_kscale(H)[:, None]
    tab_words, tab_scales = pack_weight(n((K, T)) * s, "e4m3")
    wval = n((K, H)) / np.sqrt(K) / s * u.T
    wgate_words, wgate_scales = pack_weight(1.5 * n((K, H)) / np.sqrt(K) / s, "e2m1")
    wbase_words, wbase_scales = pack_weight(n((K, H)) / np.sqrt(K) / s, "e4m3")
    gain = np.exp(0.3 * n(H)) * u[:, 0]
    wq = n((H, N)) / np.sqrt(H) / u
    return {"tab_words": tab_words, "tab_scales": tab_scales,
            "offs": striped(np.random.permutation(T)[:S]),
            "wval": wval.astype(np.float32),
            "wgate_words": wgate_words, "wgate_scales": wgate_scales,
            "wbase_words": wbase_words, "wbase_scales": wbase_scales,
            "gain": gain.astype(np.float32), "wq": wq.astype(np.float32)}

def reference(tab_words, tab_scales, offs, wval, wgate_words, wgate_scales,
              wbase_words, wbase_scales, gain, wq):
    v = unpack_weight(tab_words, tab_scales, "e4m3")[:, unstriped(offs)]
    wgate = unpack_weight(wgate_words, wgate_scales, "e2m1")
    wbase = unpack_weight(wbase_words, wbase_scales, "e4m3")
    a = mxq(f64(wval), 0, "e4m3").T @ v
    g = wgate.T @ v
    b = wbase.T @ v
    gate = 1.0 / (1.0 + np.exp(-g))
    h = a * gate - f64(gain)[:, None] * np.tanh(b)
    return mxq(f64(wq), 0, "e4m3").T @ mxq(h, 0, "e4m3")

@@ -1,0 +1,251 @@
+from contextlib import ExitStack
+
+import concourse.mybir as mybir
+
+K, T, S, H, N = 1024, 4096, 1024, 512, 256
+FLOPS = 2 * S * H * (3 * K + N)
+
+F32 = mybir.dt.float32
+BF16 = mybir.dt.bfloat16
+I32 = mybir.dt.int32
+U32 = mybir.dt.uint32
+U16 = mybir.dt.uint16
+U8 = mybir.dt.uint8
+FP8X4 = mybir.dt.float8_e4m3fn_x4
+FP4X4 = mybir.dt.float4_e2m1fn_x4
+ACT = mybir.ActivationFunctionType
+ALU = mybir.AluOpType
+
+P = 128
+PACK = 4
+PASSES = K // (P * PACK)
+HALF = 512
+GATE_COL = S
+BASE_COL = S + H
+PLANE_W = S + 2 * H
+
+
+def tile_list_replay_gated_q_kernel(tc, tab_words, tab_scales, offs, wval, wgate_words, wgate_scales,
+                                             wbase_words, wbase_scales, gain, wq, out):
+    nc = tc.nc
+    with ExitStack() as ctx:
+        keep = ctx.enter_context(tc.tile_pool(name="keep", bufs=1))
+        ring = ctx.enter_context(tc.tile_pool(name="ring", bufs=3))
+        psum = ctx.enter_context(tc.psum_pool(name="psum", bufs=1))
+
+        def bank(b):
+            return psum.tile([P, HALF], F32, name="bank%d" % b, tag="bank%d" % b)
+
+        offsets = keep.tile([P, S // 16], U16, name="offsets")
+        nc.sync.dma_start(offsets[:], offs)
+
+        tab_rows = keep.tile([P, T], U8, name="tab_rows", align_bytes=64)
+        w_rows = keep.tile([P, 2 * H], U8, name="w_rows", align_bytes=64)
+        planes = keep.tile([P, PASSES, PLANE_W], U8, name="planes", align_bytes=64)
+        nc.vector.memset(tab_rows[:].bitcast(I32), 0)
+        nc.gpsimd.memset(w_rows[:].bitcast(I32), 0)
+        nc.vector.memset(planes[:].bitcast(I32), 0)
+
+        base_raw = keep.tile([P, PASSES, H], I32, name="base_raw")
+        nc.sync.dma_start(base_raw[:], wbase_words.rearrange("a p c i -> p a (c i)").bitcast(I32))
+        nc.sync.dma_start(tab_rows[0:P:4, :].bitcast(I32), tab_scales.rearrange("a q t -> q a t").bitcast(I32))
+        nc.sync.dma_start(w_rows[0:P:4, 0:H].bitcast(I32), wgate_scales.rearrange("a q c -> q a c").bitcast(I32))
+        nc.sync.dma_start(w_rows[0:P:4, H:2 * H].bitcast(I32), wbase_scales.rearrange("a q c -> q a c").bitcast(I32))
+        gate_raw = keep.tile([P, PASSES, H // 2], I32, name="gate_raw")
+        nc.sync.dma_start(gate_raw[:], wgate_words.rearrange("a p b -> p a b").bitcast(I32))
+        tables = []
+
+        def load_table(a, tag):
+            table = keep.tile([P, T], I32, name="table%d" % a, tag=tag, align_bytes=64)
+            nc.sync.dma_start(table[:], tab_words[a].rearrange("p t i -> p (t i)").bitcast(I32))
+            tables.append(table)
+
+        load_table(0, "table0")
+
+        picked_rows = keep.tile([P, S], U8, name="picked_rows", tag="table1", align_bytes=64)
+        nc.vector.tensor_copy(picked_rows[:], tab_rows[:].indirect(offsets[:]))
+        staged = keep.tile([P, PLANE_W], U8, name="staged", tag="staging", align_bytes=64)
+        nc.vector.tensor_copy(staged[:, S:PLANE_W].rearrange("p (w t m) -> p w m t", w=2, t=PACK),
+                              w_rows[:].rearrange("p (w m t) -> p w m t", w=2, t=PACK))
+        nc.vector.tensor_copy(staged[:, 0:S].bitcast(I32), picked_rows[:].bitcast(I32))
+        for q in range(4):
+            nc.sync.dma_start(planes[32 * q:32 * q + 4].rearrange("p a c -> p (a c)").bitcast(I32),
+                              staged[32 * q:32 * q + 32:4, :].bitcast(I32))
+        load_table(1, "table1")
+
+        gate_codes = keep.tile([P, PASSES, 2 * H], U8, name="gate_codes", align_bytes=64)
+        nc.vector.tensor_copy(gate_codes[:].bitcast(U16).rearrange("p a (t m) -> p a m t", t=PACK),
+                              gate_raw[:].bitcast(U16).rearrange("p a (m t) -> p a m t", t=PACK))
+        base_codes = keep.tile([P, PASSES, H], I32, name="base_codes", align_bytes=64)
+        nc.vector.tensor_copy(base_codes[:].rearrange("p a (t m) -> p a m t", t=PACK),
+                              base_raw[:].rearrange("p a (m t) -> p a m t", t=PACK))
+
+        floats = keep.tile([P, 5 * PACK * N + 8], F32, name="floats", tag="staging", align_bytes=64)
+        gains = floats[:, 5 * PACK * N:5 * PACK * N + PACK]
+        nc.sync.dma_start(gains, gain.rearrange("(p t) -> p t", t=PACK))
+        val_pieces = [(0, 0, H), (1, 0, H // 2), (1, H // 2, H // 2)]
+        val_raw = []
+        at = 0
+        for a, c0, width in val_pieces:
+            piece = floats[:, at:at + PACK * width].rearrange("p (j c) -> p j c", j=PACK)
+            nc.sync.dma_start(piece, wval[a * 512:(a + 1) * 512, c0:c0 + width].rearrange("(p j) c -> p j c", j=PACK))
+            val_raw.append(piece)
+            at += PACK * width
+        wq_raw = floats[:, at:at + PACK * N].rearrange("p (t n) -> p t n", t=PACK)
+        nc.sync.dma_start(wq_raw, wq.rearrange("(p t) n -> p t n", t=PACK))
+
+        picked = {}
+
+        def gather(a, half):
+            words = keep.tile([P, HALF], U32, name="picked%d%d" % (a, half), align_bytes=64)
+            cols = HALF // 16
+            nc.vector.tensor_copy(words[:], tables[a][:].bitcast(U32).indirect(offsets[:, half * cols:(half + 1) * cols]))
+            picked[a, half] = words
+
+        def product(acc, codes, scales, a, c0, width):
+            half, lo = divmod(c0, HALF)
+            nc.tensor.matmul_mx(out=acc, lhsT=codes, lhsT_scale=scales,
+                                rhs=picked[a, half][:, lo:lo + width].bitcast(FP8X4),
+                                rhs_scale=planes[:, a, c0:c0 + width],
+                                start=(a == 0), stop=(a == PASSES - 1))
+
+        def gate_pass(acc, a, t, half):
+            product(acc[:], gate_codes[:, a, 2 * P * t:2 * P * (t + 1)].bitcast(FP4X4),
+                    planes[:, a, GATE_COL + P * t:GATE_COL + P * (t + 1)], a, half * HALF, HALF)
+
+        def base_pass(acc, a, t, half):
+            product(acc[:], base_codes[:, a, P * t:P * (t + 1)].bitcast(FP8X4),
+                    planes[:, a, BASE_COL + P * t:BASE_COL + P * (t + 1)], a, half * HALF, HALF)
+
+        sig = [keep.tile([P, PACK, HALF], F32, name="sig%d" % h) for h in range(2)]
+        ntanh = [keep.tile([P, PACK, HALF], F32, name="ntanh%d" % h) for h in range(2)]
+
+        def squash(g_acc, b_acc, t, half):
+            nc.scalar.activation(sig[half][:, t, :], g_acc[:], ACT.Sigmoid)
+            nc.scalar.activation(ntanh[half][:, t, :], b_acc[:], ACT.Tanh, scale=-1.0)
+
+        gather(0, 0)
+        gather(0, 1)
+        first = [(bank(2 * t), bank(2 * t + 1)) for t in range(PACK)]
+        for t in range(PACK):
+            gate_pass(first[t][0], 0, t, 0)
+            base_pass(first[t][1], 0, t, 0)
+        gather(1, 0)
+        gather(1, 1)
+        for t in range(PACK):
+            gate_pass(first[t][0], 1, t, 0)
+            base_pass(first[t][1], 1, t, 0)
+            squash(first[t][0], first[t][1], t, 0)
+
+        def second(t, b0):
+            g_acc, b_acc = bank(b0), bank(b0 + 1)
+            for a in range(PASSES):
+                gate_pass(g_acc, a, t, 1)
+            for a in range(PASSES):
+                base_pass(b_acc, a, t, 1)
+            squash(g_acc, b_acc, t, 1)
+
+        val_bf = [keep.tile([P, PACK, P, PACK], BF16, name="val_bf%d" % a, align_bytes=64) for a in range(PASSES)]
+        val_codes = [keep.tile([P, H], U32, name="val_codes%d" % a, align_bytes=64) for a in range(PASSES)]
+        val_scales = [keep.tile([P, H], U8, name="val_scales%d" % a, align_bytes=64) for a in range(PASSES)]
+
+        def cast_val(i):
+            a, c0, width = val_pieces[i]
+            m0, m1 = c0 // PACK, (c0 + width) // PACK
+            nc.vector.tensor_copy(val_bf[a][:, :, m0:m1, :].rearrange("p t m j -> p m j t"),
+                                  val_raw[i].rearrange("p j (m t) -> p m j t", t=PACK))
+
+        def quantize_val(a, t0, t1):
+            nc.vector.quantize_mx(out=val_codes[a][:, P * t0:P * t1].bitcast(FP8X4), scales=val_scales[a][:, P * t0:P * t1],
+                                  in_=val_bf[a][:, t0:t1].rearrange("p t m j -> p (t m j)"))
+
+        cast_val(0)
+        cast_val(1)
+        quantize_val(0, 0, PACK)
+        cast_val(2)
+        for t in range(PACK):
+            quantize_val(1, t, t + 1)
+
+        second(0, 0)
+        second(1, 2)
+
+        chunks = [(0, 512), (512, 256), (768, 256)]
+        h_rows = [keep.tile([P, PACK, width], BF16, name="h_rows%d" % i) for i, (c0, width) in enumerate(chunks)]
+        h_mixed = [keep.tile([P, width, PACK], BF16, name="h_mixed%d" % i, align_bytes=64) for i, (c0, width) in enumerate(chunks)]
+        h_codes = [keep.tile([P, width], U32, name="h_codes%d" % i, align_bytes=64) for i, (c0, width) in enumerate(chunks)]
+        h_scales = [keep.tile([P, width], U8, name="h_scales%d" % i, align_bytes=64) for i, (c0, width) in enumerate(chunks)]
+        gated = {}
+
+        def value(i, t0, b):
+            c0, width = chunks[i]
+            half, lo = divmod(c0, HALF)
+            count = HALF // width
+            acc = bank(b)
+            for u in range(count):
+                t = t0 + u
+                for a in range(PASSES):
+                    product(acc[:, u * width:(u + 1) * width], val_codes[a][:, P * t:P * (t + 1)].bitcast(FP8X4),
+                            val_scales[a][:, P * t:P * (t + 1)], a, c0, width)
+            prod = ring.tile([P, HALF], F32, name="prod")
+            nc.vector.tensor_tensor(prod[:].rearrange("p (u c) -> p u c", u=count), acc[:].rearrange("p (u c) -> p u c", u=count),
+                                    sig[half][:, t0:t0 + count, lo:lo + width], ALU.mult)
+            for u in range(count):
+                gated[i, t0 + u] = prod[:, u * width:(u + 1) * width]
+
+        def combine(i, t):
+            c0, width = chunks[i]
+            half, lo = divmod(c0, HALF)
+            nc.vector.scalar_tensor_tensor(h_rows[i][:, t, :], ntanh[half][:, t, lo:lo + width], gains[:, t:t + 1],
+                                           gated[i, t], ALU.mult, ALU.add)
+
+        def weave(i, copy):
+            copy(h_mixed[i][:].rearrange("p (c e) t -> p c t e", e=4), h_rows[i][:].rearrange("p t (c e) -> p c t e", e=4))
+
+        def quantize_h(i):
+            nc.vector.quantize_mx(out=h_codes[i][:].bitcast(FP8X4), scales=h_scales[i][:],
+                                  in_=h_mixed[i][:].rearrange("p c t -> p (c t)"))
+
+        wq_bf = keep.tile([P, N, PACK], BF16, name="wq_bf", align_bytes=64)
+        wq_codes = keep.tile([P, N], U32, name="wq_codes", align_bytes=64)
+        wq_scales = keep.tile([P, N], U8, name="wq_scales", align_bytes=64)
+
+        def finish(i, banks, copies):
+            c0, width = chunks[i]
+            for nt in range(N // P):
+                acc = bank(banks[nt])
+                nc.tensor.matmul_mx(out=acc[:, 0:width], lhsT=wq_codes[:, P * nt:P * (nt + 1)].bitcast(FP8X4),
+                                    lhsT_scale=wq_scales[:, P * nt:P * (nt + 1)],
+                                    rhs=h_codes[i][:].bitcast(FP8X4), rhs_scale=h_scales[i][:], start=True, stop=True)
+                result = keep.tile([P, width], F32, name="result%d%d" % (i, nt))
+                copies[nt](result[:], acc[:, 0:width])
+                nc.sync.dma_start(out[P * nt:P * (nt + 1), c0:c0 + width], result[:])
+
+        value(0, 0, 4)
+        value(0, 1, 5)
+        second(2, 6)
+        combine(0, 0)
+        value(0, 2, 4)
+        combine(0, 1)
+        value(0, 3, 5)
+        second(3, 0)
+        combine(0, 2)
+        nc.scalar.copy(wq_bf[:].rearrange("p (c e) t -> p c t e", e=4), wq_raw.rearrange("p t (c e) -> p c t e", e=4))
+        value(1, 0, 4)
+        combine(0, 3)
+        weave(0, nc.scalar.copy)
+        value(1, 2, 5)
+        nc.vector.quantize_mx(out=wq_codes[:].bitcast(FP8X4), scales=wq_scales[:], in_=wq_bf[:].rearrange("p n t -> p (n t)"))
+        for t in range(PACK):
+            combine(1, t)
+        weave(1, nc.scalar.copy)
+        value(2, 0, 4)
+        value(2, 2, 5)
+        quantize_h(0)
+        finish(0, (2, 3), (nc.scalar.copy, nc.scalar.copy))
+        for t in range(PACK):
+            combine(2, t)
+        quantize_h(1)
+        weave(2, nc.vector.tensor_copy)
+        finish(1, (6, 7), (nc.scalar.copy, nc.scalar.copy))
+        quantize_h(2)
+        finish(2, (0, 1), (nc.scalar.copy, nc.vector.tensor_copy))

@@ -20,9 +20,14 @@ P = 128
 PACK = 4
 PASSES = K // (P * PACK)
 HALF = 512
+ROWS = 32
 GATE_COL = S
 BASE_COL = S + H
 PLANE_W = S + 2 * H
+PIECE = 4096
+BASE_AT = 4 * PIECE
+GAINS_AT = 5 * PIECE
+REUSED = GAINS_AT + 64
 
 
 def tile_list_replay_gated_q_kernel(tc, tab_words, tab_scales, offs, wval, wgate_words, wgate_scales,
@@ -30,7 +35,7 @@ def tile_list_replay_gated_q_kernel(tc, tab_words, tab_scales, offs, wval, wgate
     nc = tc.nc
     with ExitStack() as ctx:
         keep = ctx.enter_context(tc.tile_pool(name="keep", bufs=1))
-        ring = ctx.enter_context(tc.tile_pool(name="ring", bufs=3))
+        reuse = ctx.enter_context(tc.tile_pool(name="reuse", bufs=1))
         psum = ctx.enter_context(tc.psum_pool(name="psum", bufs=1))
 
         def bank(b):
@@ -42,15 +47,15 @@ def tile_list_replay_gated_q_kernel(tc, tab_words, tab_scales, offs, wval, wgate
         tab_rows = keep.tile([P, T], U8, name="tab_rows", align_bytes=64)
         w_rows = keep.tile([P, 2 * H], U8, name="w_rows", align_bytes=64)
         planes = keep.tile([P, PASSES, PLANE_W], U8, name="planes", align_bytes=64)
-        nc.vector.memset(tab_rows[:].bitcast(I32), 0)
-        nc.gpsimd.memset(w_rows[:].bitcast(I32), 0)
-        nc.vector.memset(planes[:].bitcast(I32), 0)
+        nc.sync.dma_start(tab_rows[0:ROWS, :].bitcast(I32), tab_scales.rearrange("a q t -> q a t").bitcast(I32))
+        nc.sync.dma_start(w_rows[0:ROWS, 0:H].bitcast(I32), wgate_scales.rearrange("a q c -> q a c").bitcast(I32))
+        nc.sync.dma_start(w_rows[0:ROWS, H:2 * H].bitcast(I32), wbase_scales.rearrange("a q c -> q a c").bitcast(I32))
+        nc.gpsimd.memset(tab_rows[32:64, :].bitcast(I32), 0)
+        nc.vector.memset(tab_rows[64:128, :].bitcast(I32), 0)
+        for lo, hi in ((32, 64), (64, 128)):
+            nc.gpsimd.memset(w_rows[lo:hi, :].bitcast(I32), 0)
+        nc.gpsimd.memset(planes[:].bitcast(I32), 0)
 
-        base_raw = keep.tile([P, PASSES, H], I32, name="base_raw")
-        nc.sync.dma_start(base_raw[:], wbase_words.rearrange("a p c i -> p a (c i)").bitcast(I32))
-        nc.sync.dma_start(tab_rows[0:P:4, :].bitcast(I32), tab_scales.rearrange("a q t -> q a t").bitcast(I32))
-        nc.sync.dma_start(w_rows[0:P:4, 0:H].bitcast(I32), wgate_scales.rearrange("a q c -> q a c").bitcast(I32))
-        nc.sync.dma_start(w_rows[0:P:4, H:2 * H].bitcast(I32), wbase_scales.rearrange("a q c -> q a c").bitcast(I32))
         gate_raw = keep.tile([P, PASSES, H // 2], I32, name="gate_raw")
         nc.sync.dma_start(gate_raw[:], wgate_words.rearrange("a p b -> p a b").bitcast(I32))
         tables = []
@@ -64,35 +69,31 @@ def tile_list_replay_gated_q_kernel(tc, tab_words, tab_scales, offs, wval, wgate
 
         picked_rows = keep.tile([P, S], U8, name="picked_rows", tag="table1", align_bytes=64)
         nc.vector.tensor_copy(picked_rows[:], tab_rows[:].indirect(offsets[:]))
-        staged = keep.tile([P, PLANE_W], U8, name="staged", tag="staging", align_bytes=64)
-        nc.vector.tensor_copy(staged[:, S:PLANE_W].rearrange("p (w t m) -> p w m t", w=2, t=PACK),
-                              w_rows[:].rearrange("p (w m t) -> p w m t", w=2, t=PACK))
+        staged = reuse.tile([P, REUSED], U8, name="staged", align_bytes=64, offset=0)
+        nc.vector.tensor_copy(staged[:, S:PLANE_W].bitcast(U16).rearrange("p (w t m) -> p w t m", w=2, t=PACK),
+                              w_rows[:].bitcast(U16).rearrange("p (w m t) -> p w t m", w=2, t=PACK))
         nc.vector.tensor_copy(staged[:, 0:S].bitcast(I32), picked_rows[:].bitcast(I32))
         for q in range(4):
             nc.sync.dma_start(planes[32 * q:32 * q + 4].rearrange("p a c -> p (a c)").bitcast(I32),
-                              staged[32 * q:32 * q + 32:4, :].bitcast(I32))
+                              staged[8 * q:8 * q + 8, 0:PLANE_W].bitcast(I32))
         load_table(1, "table1")
 
         gate_codes = keep.tile([P, PASSES, 2 * H], U8, name="gate_codes", align_bytes=64)
-        nc.vector.tensor_copy(gate_codes[:].bitcast(U16).rearrange("p a (t m) -> p a m t", t=PACK),
-                              gate_raw[:].bitcast(U16).rearrange("p a (m t) -> p a m t", t=PACK))
-        base_codes = keep.tile([P, PASSES, H], I32, name="base_codes", align_bytes=64)
-        nc.vector.tensor_copy(base_codes[:].rearrange("p a (t m) -> p a m t", t=PACK),
-                              base_raw[:].rearrange("p a (m t) -> p a m t", t=PACK))
+        nc.vector.tensor_copy(gate_codes[:].bitcast(I32).rearrange("p a (t m) -> p a m t", t=PACK),
+                              gate_raw[:].rearrange("p a (m t) -> p a m t", t=PACK))
 
-        floats = keep.tile([P, 5 * PACK * N + 8], F32, name="floats", tag="staging", align_bytes=64)
-        gains = floats[:, 5 * PACK * N:5 * PACK * N + PACK]
-        nc.sync.dma_start(gains, gain.rearrange("(p t) -> p t", t=PACK))
-        val_pieces = [(0, 0, H), (1, 0, H // 2), (1, H // 2, H // 2)]
+        base_raw = reuse.tile([P, PASSES * H], I32, name="base_raw", align_bytes=64, offset=BASE_AT)
+        nc.sync.dma_start(base_raw[:].rearrange("p (a c) -> p a c", a=PASSES),
+                          wbase_words.rearrange("a p c i -> p a (c i)").bitcast(I32))
+        gains = reuse.tile([P, 8], F32, name="gains", align_bytes=64, offset=GAINS_AT)
+        val_pieces = [(0, 0, H // 2), (0, H // 2, H // 2), (1, 0, H // 2), (1, H // 2, H // 2)]
         val_raw = []
-        at = 0
-        for a, c0, width in val_pieces:
-            piece = floats[:, at:at + PACK * width].rearrange("p (j c) -> p j c", j=PACK)
-            nc.sync.dma_start(piece, wval[a * 512:(a + 1) * 512, c0:c0 + width].rearrange("(p j) c -> p j c", j=PACK))
+        for i, (a, c0, width) in enumerate(val_pieces):
+            piece = reuse.tile([P, PACK, width], F32, name="piece%d" % i, align_bytes=64, offset=i * PIECE)
+            nc.sync.dma_start(piece[:], wval[a * 512:(a + 1) * 512, c0:c0 + width].rearrange("(p j) c -> p j c", j=PACK))
             val_raw.append(piece)
-            at += PACK * width
-        wq_raw = floats[:, at:at + PACK * N].rearrange("p (t n) -> p t n", t=PACK)
-        nc.sync.dma_start(wq_raw, wq.rearrange("(p t) n -> p t n", t=PACK))
+        for e in range(2):
+            nc.sync.dma_start(gains[e:P:2, 0:7], gain.rearrange("(m x) -> m x", x=8)[:, e:e + 7])
 
         picked = {}
 
@@ -102,104 +103,95 @@ def tile_list_replay_gated_q_kernel(tc, tab_words, tab_scales, offs, wval, wgate
             nc.vector.tensor_copy(words[:], tables[a][:].bitcast(U32).indirect(offsets[:, half * cols:(half + 1) * cols]))
             picked[a, half] = words
 
-        def product(acc, codes, scales, a, c0, width):
-            half, lo = divmod(c0, HALF)
-            nc.tensor.matmul_mx(out=acc, lhsT=codes, lhsT_scale=scales,
-                                rhs=picked[a, half][:, lo:lo + width].bitcast(FP8X4),
-                                rhs_scale=planes[:, a, c0:c0 + width],
+        def product(acc, codes, scales, a, half):
+            nc.tensor.matmul_mx(out=acc[:], lhsT=codes, lhsT_scale=scales,
+                                rhs=picked[a, half][:].bitcast(FP8X4),
+                                rhs_scale=planes[:, a, half * HALF:(half + 1) * HALF],
                                 start=(a == 0), stop=(a == PASSES - 1))
 
         def gate_pass(acc, a, t, half):
-            product(acc[:], gate_codes[:, a, 2 * P * t:2 * P * (t + 1)].bitcast(FP4X4),
-                    planes[:, a, GATE_COL + P * t:GATE_COL + P * (t + 1)], a, half * HALF, HALF)
+            product(acc, gate_codes[:, a, 2 * P * t:2 * P * (t + 1)].bitcast(FP4X4),
+                    planes[:, a, GATE_COL + P * t:GATE_COL + P * (t + 1)], a, half)
+
+        base_codes = keep.tile([P, PASSES, H], I32, name="base_codes", align_bytes=64)
 
         def base_pass(acc, a, t, half):
-            product(acc[:], base_codes[:, a, P * t:P * (t + 1)].bitcast(FP8X4),
-                    planes[:, a, BASE_COL + P * t:BASE_COL + P * (t + 1)], a, half * HALF, HALF)
-
-        sig = [keep.tile([P, PACK, HALF], F32, name="sig%d" % h) for h in range(2)]
-        ntanh = [keep.tile([P, PACK, HALF], F32, name="ntanh%d" % h) for h in range(2)]
-
-        def squash(g_acc, b_acc, t, half):
-            nc.scalar.activation(sig[half][:, t, :], g_acc[:], ACT.Sigmoid)
-            nc.scalar.activation(ntanh[half][:, t, :], b_acc[:], ACT.Tanh, scale=-1.0)
-
-        gather(0, 0)
-        gather(0, 1)
-        first = [(bank(2 * t), bank(2 * t + 1)) for t in range(PACK)]
-        for t in range(PACK):
-            gate_pass(first[t][0], 0, t, 0)
-            base_pass(first[t][1], 0, t, 0)
-        gather(1, 0)
-        gather(1, 1)
-        for t in range(PACK):
-            gate_pass(first[t][0], 1, t, 0)
-            base_pass(first[t][1], 1, t, 0)
-            squash(first[t][0], first[t][1], t, 0)
-
-        def second(t, b0):
-            g_acc, b_acc = bank(b0), bank(b0 + 1)
-            for a in range(PASSES):
-                gate_pass(g_acc, a, t, 1)
-            for a in range(PASSES):
-                base_pass(b_acc, a, t, 1)
-            squash(g_acc, b_acc, t, 1)
+            product(acc, base_codes[:, a, P * t:P * (t + 1)].bitcast(FP8X4),
+                    planes[:, a, BASE_COL + P * t:BASE_COL + P * (t + 1)], a, half)
 
         val_bf = [keep.tile([P, PACK, P, PACK], BF16, name="val_bf%d" % a, align_bytes=64) for a in range(PASSES)]
         val_codes = [keep.tile([P, H], U32, name="val_codes%d" % a, align_bytes=64) for a in range(PASSES)]
         val_scales = [keep.tile([P, H], U8, name="val_scales%d" % a, align_bytes=64) for a in range(PASSES)]
 
+        def val_pass(acc, a, t, half):
+            product(acc, val_codes[a][:, P * t:P * (t + 1)].bitcast(FP8X4), val_scales[a][:, P * t:P * (t + 1)], a, half)
+
         def cast_val(i):
             a, c0, width = val_pieces[i]
             m0, m1 = c0 // PACK, (c0 + width) // PACK
-            nc.vector.tensor_copy(val_bf[a][:, :, m0:m1, :].rearrange("p t m j -> p m j t"),
-                                  val_raw[i].rearrange("p j (m t) -> p m j t", t=PACK))
+            nc.vector.tensor_copy(val_bf[a][:, :, m0:m1, :].rearrange("p t (m e) j -> p m t j e", e=2),
+                                  val_raw[i][:].rearrange("p j (m t e) -> p m t j e", t=PACK, e=2))
 
         def quantize_val(a, t0, t1):
             nc.vector.quantize_mx(out=val_codes[a][:, P * t0:P * t1].bitcast(FP8X4), scales=val_scales[a][:, P * t0:P * t1],
                                   in_=val_bf[a][:, t0:t1].rearrange("p t m j -> p (t m j)"))
 
-        cast_val(0)
-        cast_val(1)
-        quantize_val(0, 0, PACK)
-        cast_val(2)
-        for t in range(PACK):
-            quantize_val(1, t, t + 1)
+        sig = [keep.tile([P, PACK, HALF], F32, name="sig%d" % h) for h in range(2)]
+        squashed = [keep.tile([P, PACK, HALF], F32, name="squashed%d" % h) for h in range(2)]
+        baseline = [keep.tile([P, PACK, HALF], F32, name="baseline%d" % h) for h in range(2)]
+        gated = [keep.tile([P, PACK, HALF], F32, name="gated%d" % h) for h in range(2)]
 
-        second(0, 0)
-        second(1, 2)
+        gate_acc = {(half, t): bank(PACK * half + t) for half in range(2) for t in range(PACK)}
+        for half in range(2):
+            gather(0, half)
+            for t in range(PACK):
+                gate_pass(gate_acc[half, t], 0, t, half)
+        for half in range(2):
+            gather(1, half)
+            for t in range(PACK):
+                gate_pass(gate_acc[half, t], 1, t, half)
+        nc.vector.tensor_copy(base_codes[:].rearrange("p a (t m e) -> p a t m e", t=PACK, e=2),
+                              base_raw[:].rearrange("p (a m t e) -> p a t m e", a=PASSES, t=PACK, e=2))
+
+        wq_raw = reuse.tile([P, PACK, N], F32, name="wq_raw", align_bytes=64, offset=BASE_AT)
+        for e in range(2):
+            nc.sync.dma_start(wq_raw[e:P:2], wq.rearrange("(m t e) n -> e m t n", t=PACK, e=2)[e])
+
+        def sigmoids(half):
+            for t in range(PACK):
+                nc.scalar.activation(sig[half][:, t, :], gate_acc[half, t][:], ACT.Sigmoid)
+
+        def tanhs(half):
+            for t in range(PACK):
+                acc = bank(PACK * half + t)
+                for a in range(PASSES):
+                    base_pass(acc, a, t, half)
+                nc.scalar.activation(squashed[half][:, t, :], acc[:], ACT.Tanh)
+
+        def scale_baseline(half, lo, width):
+            for t in range(PACK):
+                nc.scalar.activation(baseline[half][:, t, lo:lo + width], squashed[half][:, t, lo:lo + width],
+                                     ACT.Copy, scale=gains[:, 2 * t:2 * t + 1])
+
+        def values(half):
+            for t in range(PACK):
+                acc = bank(t)
+                for a in range(PASSES):
+                    val_pass(acc, a, t, half)
+                nc.vector.tensor_tensor(gated[half][:, t, :], acc[:], sig[half][:, t, :], ALU.mult)
 
         chunks = [(0, 512), (512, 256), (768, 256)]
-        h_rows = [keep.tile([P, PACK, width], BF16, name="h_rows%d" % i) for i, (c0, width) in enumerate(chunks)]
         h_mixed = [keep.tile([P, width, PACK], BF16, name="h_mixed%d" % i, align_bytes=64) for i, (c0, width) in enumerate(chunks)]
         h_codes = [keep.tile([P, width], U32, name="h_codes%d" % i, align_bytes=64) for i, (c0, width) in enumerate(chunks)]
         h_scales = [keep.tile([P, width], U8, name="h_scales%d" % i, align_bytes=64) for i, (c0, width) in enumerate(chunks)]
-        gated = {}
 
-        def value(i, t0, b):
+        def subtract(i):
             c0, width = chunks[i]
             half, lo = divmod(c0, HALF)
-            count = HALF // width
-            acc = bank(b)
-            for u in range(count):
-                t = t0 + u
-                for a in range(PASSES):
-                    product(acc[:, u * width:(u + 1) * width], val_codes[a][:, P * t:P * (t + 1)].bitcast(FP8X4),
-                            val_scales[a][:, P * t:P * (t + 1)], a, c0, width)
-            prod = ring.tile([P, HALF], F32, name="prod")
-            nc.vector.tensor_tensor(prod[:].rearrange("p (u c) -> p u c", u=count), acc[:].rearrange("p (u c) -> p u c", u=count),
-                                    sig[half][:, t0:t0 + count, lo:lo + width], ALU.mult)
-            for u in range(count):
-                gated[i, t0 + u] = prod[:, u * width:(u + 1) * width]
-
-        def combine(i, t):
-            c0, width = chunks[i]
-            half, lo = divmod(c0, HALF)
-            nc.vector.scalar_tensor_tensor(h_rows[i][:, t, :], ntanh[half][:, t, lo:lo + width], gains[:, t:t + 1],
-                                           gated[i, t], ALU.mult, ALU.add)
-
-        def weave(i, copy):
-            copy(h_mixed[i][:].rearrange("p (c e) t -> p c t e", e=4), h_rows[i][:].rearrange("p t (c e) -> p c t e", e=4))
+            nc.vector.tensor_tensor(h_mixed[i][:].rearrange("p (c e) t -> p c t e", e=2),
+                                    gated[half][:, :, lo:lo + width].rearrange("p t (c e) -> p c t e", e=2),
+                                    baseline[half][:, :, lo:lo + width].rearrange("p t (c e) -> p c t e", e=2),
+                                    ALU.subtract)
 
         def quantize_h(i):
             nc.vector.quantize_mx(out=h_codes[i][:].bitcast(FP8X4), scales=h_scales[i][:],
@@ -211,41 +203,39 @@ def tile_list_replay_gated_q_kernel(tc, tab_words, tab_scales, offs, wval, wgate
 
         def finish(i, banks, copies):
             c0, width = chunks[i]
+            result = keep.tile([P, N // P, width], F32, name="result%d" % i)
             for nt in range(N // P):
                 acc = bank(banks[nt])
                 nc.tensor.matmul_mx(out=acc[:, 0:width], lhsT=wq_codes[:, P * nt:P * (nt + 1)].bitcast(FP8X4),
                                     lhsT_scale=wq_scales[:, P * nt:P * (nt + 1)],
                                     rhs=h_codes[i][:].bitcast(FP8X4), rhs_scale=h_scales[i][:], start=True, stop=True)
-                result = keep.tile([P, width], F32, name="result%d%d" % (i, nt))
-                copies[nt](result[:], acc[:, 0:width])
-                nc.sync.dma_start(out[P * nt:P * (nt + 1), c0:c0 + width], result[:])
+                copies[nt](result[:, nt, :], acc[:, 0:width])
+            nc.sync.dma_start(out[:, c0:c0 + width].rearrange("(u p) c -> p u c", p=P), result[:])
 
-        value(0, 0, 4)
-        value(0, 1, 5)
-        second(2, 6)
-        combine(0, 0)
-        value(0, 2, 4)
-        combine(0, 1)
-        value(0, 3, 5)
-        second(3, 0)
-        combine(0, 2)
-        nc.scalar.copy(wq_bf[:].rearrange("p (c e) t -> p c t e", e=4), wq_raw.rearrange("p t (c e) -> p c t e", e=4))
-        value(1, 0, 4)
-        combine(0, 3)
-        weave(0, nc.scalar.copy)
-        value(1, 2, 5)
-        nc.vector.quantize_mx(out=wq_codes[:].bitcast(FP8X4), scales=wq_scales[:], in_=wq_bf[:].rearrange("p n t -> p (n t)"))
+        sigmoids(0)
+        tanhs(0)
+        cast_val(0)
+        cast_val(1)
+        quantize_val(0, 0, PACK)
+        cast_val(2)
+        cast_val(3)
         for t in range(PACK):
-            combine(1, t)
-        weave(1, nc.scalar.copy)
-        value(2, 0, 4)
-        value(2, 2, 5)
+            quantize_val(1, t, t + 1)
+        scale_baseline(0, 0, HALF)
+        values(0)
+        sigmoids(1)
+        tanhs(1)
+        subtract(0)
+        nc.scalar.copy(wq_bf[:].rearrange("p (c e) t -> p c t e", e=4), wq_raw[:].rearrange("p t (c e) -> p c t e", e=4))
+        values(1)
         quantize_h(0)
-        finish(0, (2, 3), (nc.scalar.copy, nc.scalar.copy))
-        for t in range(PACK):
-            combine(2, t)
+        nc.vector.quantize_mx(out=wq_codes[:].bitcast(FP8X4), scales=wq_scales[:], in_=wq_bf[:].rearrange("p n t -> p (n t)"))
+        scale_baseline(1, 0, 256)
+        scale_baseline(1, 256, 256)
+        subtract(1)
+        finish(0, (4, 5), (nc.scalar.copy, nc.scalar.copy))
+        subtract(2)
         quantize_h(1)
-        weave(2, nc.vector.tensor_copy)
         finish(1, (6, 7), (nc.scalar.copy, nc.scalar.copy))
         quantize_h(2)
         finish(2, (0, 1), (nc.scalar.copy, nc.vector.tensor_copy))

@@ -27,7 +27,8 @@ PLANE_W = S + 2 * H
 PIECE = 4096
 BASE_AT = 4 * PIECE
 GAINS_AT = 5 * PIECE
-REUSED = GAINS_AT + 64
+TABLE_AT = GAINS_AT + 64
+REUSED = TABLE_AT + 4 * T
 
 
 def tile_list_replay_gated_q_kernel(tc, tab_words, tab_scales, offs, wval, wgate_words, wgate_scales,
@@ -46,37 +47,42 @@ def tile_list_replay_gated_q_kernel(tc, tab_words, tab_scales, offs, wval, wgate
 
         tab_rows = keep.tile([P, T], U8, name="tab_rows", align_bytes=64)
         w_rows = keep.tile([P, 2 * H], U8, name="w_rows", align_bytes=64)
-        planes = keep.tile([P, PASSES, PLANE_W], U8, name="planes", align_bytes=64)
-        nc.sync.dma_start(tab_rows[0:ROWS, :].bitcast(I32), tab_scales.rearrange("a q t -> q a t").bitcast(I32))
-        nc.sync.dma_start(w_rows[0:ROWS, 0:H].bitcast(I32), wgate_scales.rearrange("a q c -> q a c").bitcast(I32))
-        nc.sync.dma_start(w_rows[0:ROWS, H:2 * H].bitcast(I32), wbase_scales.rearrange("a q c -> q a c").bitcast(I32))
+        planes = [keep.tile([P, PLANE_W], U8, name="planes%d" % a, align_bytes=64) for a in range(PASSES)]
+        nc.sync.dma_start(tab_rows[0:ROWS, :].bitcast(I32), tab_scales.rearrange("a q t -> (a q) t").bitcast(I32))
+        nc.sync.dma_start(w_rows[0:ROWS, 0:H].bitcast(I32), wgate_scales.rearrange("a q c -> (a q) c").bitcast(I32))
+        nc.sync.dma_start(w_rows[0:ROWS, H:2 * H].bitcast(I32), wbase_scales.rearrange("a q c -> (a q) c").bitcast(I32))
         nc.gpsimd.memset(tab_rows[32:64, :].bitcast(I32), 0)
         nc.vector.memset(tab_rows[64:128, :].bitcast(I32), 0)
         for lo, hi in ((32, 64), (64, 128)):
             nc.gpsimd.memset(w_rows[lo:hi, :].bitcast(I32), 0)
-        nc.gpsimd.memset(planes[:].bitcast(I32), 0)
+        for a in range(PASSES):
+            nc.gpsimd.memset(planes[a][:].bitcast(I32), 0)
 
         gate_raw = keep.tile([P, PASSES, H // 2], I32, name="gate_raw")
         nc.sync.dma_start(gate_raw[:], wgate_words.rearrange("a p b -> p a b").bitcast(I32))
         tables = []
 
-        def load_table(a, tag):
-            table = keep.tile([P, T], I32, name="table%d" % a, tag=tag, align_bytes=64)
+        def load_table(a, table):
             nc.sync.dma_start(table[:], tab_words[a].rearrange("p t i -> p (t i)").bitcast(I32))
             tables.append(table)
 
-        load_table(0, "table0")
+        load_table(0, keep.tile([P, T], I32, name="table0", align_bytes=64))
 
-        picked_rows = keep.tile([P, S], U8, name="picked_rows", tag="table1", align_bytes=64)
-        nc.vector.tensor_copy(picked_rows[:], tab_rows[:].indirect(offsets[:]))
-        staged = reuse.tile([P, REUSED], U8, name="staged", align_bytes=64, offset=0)
+        picked_rows = reuse.tile([P, REUSED], U8, name="picked_rows", align_bytes=64, offset=0)
+        nc.vector.tensor_copy(picked_rows[:, 0:S], tab_rows[:].indirect(offsets[:]))
+        staged = keep.tile([P, PLANE_W], U8, name="staged", align_bytes=64)
         nc.vector.tensor_copy(staged[:, S:PLANE_W].bitcast(U16).rearrange("p (w t m) -> p w t m", w=2, t=PACK),
                               w_rows[:].bitcast(U16).rearrange("p (w m t) -> p w t m", w=2, t=PACK))
-        nc.vector.tensor_copy(staged[:, 0:S].bitcast(I32), picked_rows[:].bitcast(I32))
-        for q in range(4):
-            nc.sync.dma_start(planes[32 * q:32 * q + 4].rearrange("p a c -> p (a c)").bitcast(I32),
-                              staged[8 * q:8 * q + 8, 0:PLANE_W].bitcast(I32))
-        load_table(1, "table1")
+        nc.vector.tensor_copy(staged[:, 0:S].bitcast(I32), picked_rows[:, 0:S].bitcast(I32))
+
+        def move_planes(a):
+            for r in range(4):
+                nc.sync.dma_start(planes[a][r:P:32, :].bitcast(I32),
+                                  staged[16 * a + r:16 * a + 16:4, 0:PLANE_W].bitcast(I32))
+
+        move_planes(0)
+        load_table(1, reuse.tile([P, T], I32, name="table1", align_bytes=64, offset=TABLE_AT))
+        move_planes(1)
 
         gate_codes = keep.tile([P, PASSES, 2 * H], U8, name="gate_codes", align_bytes=64)
         nc.vector.tensor_copy(gate_codes[:].bitcast(I32).rearrange("p a (t m) -> p a m t", t=PACK),
@@ -86,14 +92,14 @@ def tile_list_replay_gated_q_kernel(tc, tab_words, tab_scales, offs, wval, wgate
         nc.sync.dma_start(base_raw[:].rearrange("p (a c) -> p a c", a=PASSES),
                           wbase_words.rearrange("a p c i -> p a (c i)").bitcast(I32))
         gains = reuse.tile([P, 8], F32, name="gains", align_bytes=64, offset=GAINS_AT)
+        for e in range(2):
+            nc.sync.dma_start(gains[e:P:2, 0:7], gain.rearrange("(m x) -> m x", x=8)[:, e:e + 7])
         val_pieces = [(0, 0, H // 2), (0, H // 2, H // 2), (1, 0, H // 2), (1, H // 2, H // 2)]
         val_raw = []
         for i, (a, c0, width) in enumerate(val_pieces):
             piece = reuse.tile([P, PACK, width], F32, name="piece%d" % i, align_bytes=64, offset=i * PIECE)
             nc.sync.dma_start(piece[:], wval[a * 512:(a + 1) * 512, c0:c0 + width].rearrange("(p j) c -> p j c", j=PACK))
             val_raw.append(piece)
-        for e in range(2):
-            nc.sync.dma_start(gains[e:P:2, 0:7], gain.rearrange("(m x) -> m x", x=8)[:, e:e + 7])
 
         picked = {}
 
@@ -106,18 +112,18 @@ def tile_list_replay_gated_q_kernel(tc, tab_words, tab_scales, offs, wval, wgate
         def product(acc, codes, scales, a, half):
             nc.tensor.matmul_mx(out=acc[:], lhsT=codes, lhsT_scale=scales,
                                 rhs=picked[a, half][:].bitcast(FP8X4),
-                                rhs_scale=planes[:, a, half * HALF:(half + 1) * HALF],
+                                rhs_scale=planes[a][:, half * HALF:(half + 1) * HALF],
                                 start=(a == 0), stop=(a == PASSES - 1))
 
         def gate_pass(acc, a, t, half):
             product(acc, gate_codes[:, a, 2 * P * t:2 * P * (t + 1)].bitcast(FP4X4),
-                    planes[:, a, GATE_COL + P * t:GATE_COL + P * (t + 1)], a, half)
+                    planes[a][:, GATE_COL + P * t:GATE_COL + P * (t + 1)], a, half)
 
         base_codes = keep.tile([P, PASSES, H], I32, name="base_codes", align_bytes=64)
 
         def base_pass(acc, a, t, half):
             product(acc, base_codes[:, a, P * t:P * (t + 1)].bitcast(FP8X4),
-                    planes[:, a, BASE_COL + P * t:BASE_COL + P * (t + 1)], a, half)
+                    planes[a][:, BASE_COL + P * t:BASE_COL + P * (t + 1)], a, half)
 
         val_bf = [keep.tile([P, PACK, P, PACK], BF16, name="val_bf%d" % a, align_bytes=64) for a in range(PASSES)]
         val_codes = [keep.tile([P, H], U32, name="val_codes%d" % a, align_bytes=64) for a in range(PASSES)]
@@ -163,7 +169,7 @@ def tile_list_replay_gated_q_kernel(tc, tab_words, tab_scales, offs, wval, wgate
 
         def tanhs(half):
             for t in range(PACK):
-                acc = bank(PACK * half + t)
+                acc = bank(t)
                 for a in range(PASSES):
                     base_pass(acc, a, t, half)
                 nc.scalar.activation(squashed[half][:, t, :], acc[:], ACT.Tanh)
@@ -175,7 +181,7 @@ def tile_list_replay_gated_q_kernel(tc, tab_words, tab_scales, offs, wval, wgate
 
         def values(half):
             for t in range(PACK):
-                acc = bank(t)
+                acc = bank(PACK * half + t)
                 for a in range(PASSES):
                     val_pass(acc, a, t, half)
                 nc.vector.tensor_tensor(gated[half][:, t, :], acc[:], sig[half][:, t, :], ALU.mult)
@@ -226,16 +232,16 @@ def tile_list_replay_gated_q_kernel(tc, tab_words, tab_scales, offs, wval, wgate
         sigmoids(1)
         tanhs(1)
         subtract(0)
-        nc.scalar.copy(wq_bf[:].rearrange("p (c e) t -> p c t e", e=4), wq_raw[:].rearrange("p t (c e) -> p c t e", e=4))
+        nc.vector.tensor_copy(wq_bf[:].rearrange("p (c e) t -> p c t e", e=2), wq_raw[:].rearrange("p t (c e) -> p c t e", e=2))
         values(1)
         quantize_h(0)
         nc.vector.quantize_mx(out=wq_codes[:].bitcast(FP8X4), scales=wq_scales[:], in_=wq_bf[:].rearrange("p n t -> p (n t)"))
         scale_baseline(1, 0, 256)
         scale_baseline(1, 256, 256)
         subtract(1)
-        finish(0, (4, 5), (nc.scalar.copy, nc.scalar.copy))
+        finish(0, (0, 1), (nc.scalar.copy, nc.scalar.copy))
         subtract(2)
         quantize_h(1)
-        finish(1, (6, 7), (nc.scalar.copy, nc.scalar.copy))
+        finish(1, (2, 3), (nc.scalar.copy, nc.scalar.copy))
         quantize_h(2)
-        finish(2, (0, 1), (nc.scalar.copy, nc.vector.tensor_copy))
+        finish(2, (4, 5), (nc.scalar.copy, nc.vector.tensor_copy))

@@ -24,9 +24,9 @@ ROWS = 32
 GATE_COL = S
 BASE_COL = S + H
 PLANE_W = S + 2 * H
-PIECE = 4096
-BASE_AT = 4 * PIECE
-GAINS_AT = 5 * PIECE
+PIECE = 4 * PACK * H
+BASE_AT = PASSES * PIECE
+GAINS_AT = BASE_AT + 4 * PASSES * H
 TABLE_AT = GAINS_AT + 64
 REUSED = TABLE_AT + 4 * T
 
@@ -46,17 +46,14 @@ def tile_list_replay_gated_q_kernel(tc, tab_words, tab_scales, offs, wval, wgate
         nc.sync.dma_start(offsets[:], offs)
 
         tab_rows = keep.tile([P, T], U8, name="tab_rows", align_bytes=64)
-        w_rows = keep.tile([P, 2 * H], U8, name="w_rows", align_bytes=64)
-        planes = [keep.tile([P, PLANE_W], U8, name="planes%d" % a, align_bytes=64) for a in range(PASSES)]
-        nc.sync.dma_start(tab_rows[0:ROWS, :].bitcast(I32), tab_scales.rearrange("a q t -> (a q) t").bitcast(I32))
-        nc.sync.dma_start(w_rows[0:ROWS, 0:H].bitcast(I32), wgate_scales.rearrange("a q c -> (a q) c").bitcast(I32))
-        nc.sync.dma_start(w_rows[0:ROWS, H:2 * H].bitcast(I32), wbase_scales.rearrange("a q c -> (a q) c").bitcast(I32))
-        nc.gpsimd.memset(tab_rows[32:64, :].bitcast(I32), 0)
-        nc.vector.memset(tab_rows[64:128, :].bitcast(I32), 0)
+        w_rows = keep.tile([ROWS, 2 * H], U8, name="w_rows", align_bytes=64)
+        planes = keep.tile([P, PASSES, PLANE_W], U8, name="planes", align_bytes=64)
+        nc.sync.dma_start(w_rows[0:ROWS, 0:H].bitcast(I32), wgate_scales.rearrange("a q c -> q a c").bitcast(I32))
+        nc.sync.dma_start(w_rows[0:ROWS, H:2 * H].bitcast(I32), wbase_scales.rearrange("a q c -> q a c").bitcast(I32))
+        nc.sync.dma_start(tab_rows[0:ROWS, :].bitcast(I32), tab_scales.rearrange("a q t -> q a t").bitcast(I32))
         for lo, hi in ((32, 64), (64, 128)):
-            nc.gpsimd.memset(w_rows[lo:hi, :].bitcast(I32), 0)
-        for a in range(PASSES):
-            nc.gpsimd.memset(planes[a][:].bitcast(I32), 0)
+            nc.vector.memset(tab_rows[lo:hi, :].bitcast(I32), 0)
+        nc.gpsimd.memset(planes[:].bitcast(I32), 0)
 
         gate_raw = keep.tile([P, PASSES, H // 2], I32, name="gate_raw")
         nc.sync.dma_start(gate_raw[:], wgate_words.rearrange("a p b -> p a b").bitcast(I32))
@@ -68,21 +65,16 @@ def tile_list_replay_gated_q_kernel(tc, tab_words, tab_scales, offs, wval, wgate
 
         load_table(0, keep.tile([P, T], I32, name="table0", align_bytes=64))
 
-        picked_rows = reuse.tile([P, REUSED], U8, name="picked_rows", align_bytes=64, offset=0)
-        nc.vector.tensor_copy(picked_rows[:, 0:S], tab_rows[:].indirect(offsets[:]))
-        staged = keep.tile([P, PLANE_W], U8, name="staged", align_bytes=64)
+        staged = keep.tile([ROWS, PLANE_W], U8, name="staged", align_bytes=64)
         nc.vector.tensor_copy(staged[:, S:PLANE_W].bitcast(U16).rearrange("p (w t m) -> p w t m", w=2, t=PACK),
                               w_rows[:].bitcast(U16).rearrange("p (w m t) -> p w t m", w=2, t=PACK))
-        nc.vector.tensor_copy(staged[:, 0:S].bitcast(I32), picked_rows[:, 0:S].bitcast(I32))
-
-        def move_planes(a):
-            for r in range(4):
-                nc.sync.dma_start(planes[a][r:P:32, :].bitcast(I32),
-                                  staged[16 * a + r:16 * a + 16:4, 0:PLANE_W].bitcast(I32))
-
-        move_planes(0)
+        picked_rows = reuse.tile([P, REUSED], U8, name="picked_rows", align_bytes=64, offset=0)
+        nc.vector.tensor_copy(picked_rows[:, 0:S], tab_rows[:].indirect(offsets[:]))
+        nc.vector.tensor_copy(staged[:, 0:S].bitcast(I32), picked_rows[0:ROWS, 0:S].bitcast(I32))
+        for q in range(4):
+            nc.sync.dma_start(planes[32 * q:32 * q + 4].rearrange("p a c -> p (a c)").bitcast(I32),
+                              staged[8 * q:8 * q + 8, :].bitcast(I32))
         load_table(1, reuse.tile([P, T], I32, name="table1", align_bytes=64, offset=TABLE_AT))
-        move_planes(1)
 
         gate_codes = keep.tile([P, PASSES, 2 * H], U8, name="gate_codes", align_bytes=64)
         nc.vector.tensor_copy(gate_codes[:].bitcast(I32).rearrange("p a (t m) -> p a m t", t=PACK),
@@ -92,14 +84,14 @@ def tile_list_replay_gated_q_kernel(tc, tab_words, tab_scales, offs, wval, wgate
         nc.sync.dma_start(base_raw[:].rearrange("p (a c) -> p a c", a=PASSES),
                           wbase_words.rearrange("a p c i -> p a (c i)").bitcast(I32))
         gains = reuse.tile([P, 8], F32, name="gains", align_bytes=64, offset=GAINS_AT)
-        for e in range(2):
-            nc.sync.dma_start(gains[e:P:2, 0:7], gain.rearrange("(m x) -> m x", x=8)[:, e:e + 7])
-        val_pieces = [(0, 0, H // 2), (0, H // 2, H // 2), (1, 0, H // 2), (1, H // 2, H // 2)]
+        val_pieces = [(0, 0, H), (1, 0, H // 2), (1, H // 2, H // 2)]
         val_raw = []
         for i, (a, c0, width) in enumerate(val_pieces):
-            piece = reuse.tile([P, PACK, width], F32, name="piece%d" % i, align_bytes=64, offset=i * PIECE)
+            piece = reuse.tile([P, PACK, width], F32, name="piece%d" % i, align_bytes=64, offset=a * PIECE + 16 * c0)
             nc.sync.dma_start(piece[:], wval[a * 512:(a + 1) * 512, c0:c0 + width].rearrange("(p j) c -> p j c", j=PACK))
             val_raw.append(piece)
+        for e in range(2):
+            nc.sync.dma_start(gains[e:P:2, 0:7], gain.rearrange("(m x) -> m x", x=8)[:, e:e + 7])
 
         picked = {}
 
@@ -109,28 +101,29 @@ def tile_list_replay_gated_q_kernel(tc, tab_words, tab_scales, offs, wval, wgate
             nc.vector.tensor_copy(words[:], tables[a][:].bitcast(U32).indirect(offsets[:, half * cols:(half + 1) * cols]))
             picked[a, half] = words
 
-        def product(acc, codes, scales, a, half):
+        def product(acc, codes, scales, a, half, first=0):
             nc.tensor.matmul_mx(out=acc[:], lhsT=codes, lhsT_scale=scales,
                                 rhs=picked[a, half][:].bitcast(FP8X4),
-                                rhs_scale=planes[a][:, half * HALF:(half + 1) * HALF],
-                                start=(a == 0), stop=(a == PASSES - 1))
+                                rhs_scale=planes[:, a, half * HALF:(half + 1) * HALF],
+                                start=(a == first), stop=(a != first))
 
         def gate_pass(acc, a, t, half):
             product(acc, gate_codes[:, a, 2 * P * t:2 * P * (t + 1)].bitcast(FP4X4),
-                    planes[a][:, GATE_COL + P * t:GATE_COL + P * (t + 1)], a, half)
+                    planes[:, a, GATE_COL + P * t:GATE_COL + P * (t + 1)], a, half)
 
         base_codes = keep.tile([P, PASSES, H], I32, name="base_codes", align_bytes=64)
 
         def base_pass(acc, a, t, half):
             product(acc, base_codes[:, a, P * t:P * (t + 1)].bitcast(FP8X4),
-                    planes[a][:, BASE_COL + P * t:BASE_COL + P * (t + 1)], a, half)
+                    planes[:, a, BASE_COL + P * t:BASE_COL + P * (t + 1)], a, half)
 
-        val_bf = [keep.tile([P, PACK, P, PACK], BF16, name="val_bf%d" % a, align_bytes=64) for a in range(PASSES)]
+        val_bf = [keep.tile([P, PACK, P, PACK], BF16, name="val_bf%d" % a, tag="val_bf%d" % a, align_bytes=64) for a in range(PASSES)]
         val_codes = [keep.tile([P, H], U32, name="val_codes%d" % a, align_bytes=64) for a in range(PASSES)]
         val_scales = [keep.tile([P, H], U8, name="val_scales%d" % a, align_bytes=64) for a in range(PASSES)]
 
-        def val_pass(acc, a, t, half):
-            product(acc, val_codes[a][:, P * t:P * (t + 1)].bitcast(FP8X4), val_scales[a][:, P * t:P * (t + 1)], a, half)
+        def val_pass(acc, a, t, half, first):
+            product(acc, val_codes[a][:, P * t:P * (t + 1)].bitcast(FP8X4), val_scales[a][:, P * t:P * (t + 1)], a, half,
+                    first)
 
         def cast_val(i):
             a, c0, width = val_pieces[i]
@@ -144,7 +137,8 @@ def tile_list_replay_gated_q_kernel(tc, tab_words, tab_scales, offs, wval, wgate
 
         sig = [keep.tile([P, PACK, HALF], F32, name="sig%d" % h) for h in range(2)]
         squashed = [keep.tile([P, PACK, HALF], F32, name="squashed%d" % h) for h in range(2)]
-        baseline = [keep.tile([P, PACK, HALF], F32, name="baseline%d" % h) for h in range(2)]
+        baseline = [keep.tile([P, PACK, HALF], F32, name="baseline0", tag="val_bf1", align_bytes=64),
+                    keep.tile([P, PACK, HALF], F32, name="baseline1")]
         gated = [keep.tile([P, PACK, HALF], F32, name="gated%d" % h) for h in range(2)]
 
         gate_acc = {(half, t): bank(PACK * half + t) for half in range(2) for t in range(PACK)}
@@ -163,30 +157,40 @@ def tile_list_replay_gated_q_kernel(tc, tab_words, tab_scales, offs, wval, wgate
         for e in range(2):
             nc.sync.dma_start(wq_raw[e:P:2], wq.rearrange("(m t e) n -> e m t n", t=PACK, e=2)[e])
 
-        def sigmoids(half):
-            for t in range(PACK):
+        def sigmoids(half, slices):
+            for t in slices:
                 nc.scalar.activation(sig[half][:, t, :], gate_acc[half, t][:], ACT.Sigmoid)
 
-        def tanhs(half):
-            for t in range(PACK):
-                acc = bank(t)
-                for a in range(PASSES):
-                    base_pass(acc, a, t, half)
-                nc.scalar.activation(squashed[half][:, t, :], acc[:], ACT.Tanh)
+        base_acc = {}
 
-        def scale_baseline(half, lo, width):
+        def bases(half, slices):
+            for t in slices:
+                base_acc[half, t] = bank(PACK * half + t)
+                for a in range(PASSES):
+                    base_pass(base_acc[half, t], a, t, half)
+
+        def tanhs(half, slices):
+            for t in slices:
+                nc.scalar.activation(squashed[half][:, t, :], base_acc[half, t][:], ACT.Tanh)
+
+        def scale_baseline(half):
+            for t in range(PACK):
+                nc.gpsimd.tensor_scalar(baseline[half][:, t, :], squashed[half][:, t, :], gains[:, 2 * t:2 * t + 1], 0.0,
+                                        ALU.mult, ALU.add)
+
+        def scale_baseline_part(half, lo, width):
             for t in range(PACK):
                 nc.scalar.activation(baseline[half][:, t, lo:lo + width], squashed[half][:, t, lo:lo + width],
                                      ACT.Copy, scale=gains[:, 2 * t:2 * t + 1])
 
-        def values(half):
-            for t in range(PACK):
-                acc = bank(PACK * half + t)
-                for a in range(PASSES):
-                    val_pass(acc, a, t, half)
+        def values(half, slices):
+            for t in slices:
+                acc = bank(t)
+                for a in (1, 0):
+                    val_pass(acc, a, t, half, 1)
                 nc.vector.tensor_tensor(gated[half][:, t, :], acc[:], sig[half][:, t, :], ALU.mult)
 
-        chunks = [(0, 512), (512, 256), (768, 256)]
+        chunks = [(0, 512), (512, 256), (768, 128), (896, 128)]
         h_mixed = [keep.tile([P, width, PACK], BF16, name="h_mixed%d" % i, align_bytes=64) for i, (c0, width) in enumerate(chunks)]
         h_codes = [keep.tile([P, width], U32, name="h_codes%d" % i, align_bytes=64) for i, (c0, width) in enumerate(chunks)]
         h_scales = [keep.tile([P, width], U8, name="h_scales%d" % i, align_bytes=64) for i, (c0, width) in enumerate(chunks)]
@@ -218,30 +222,38 @@ def tile_list_replay_gated_q_kernel(tc, tab_words, tab_scales, offs, wval, wgate
                 copies[nt](result[:, nt, :], acc[:, 0:width])
             nc.sync.dma_start(out[:, c0:c0 + width].rearrange("(u p) c -> p u c", p=P), result[:])
 
-        sigmoids(0)
-        tanhs(0)
+        early, late = (0, 1), (2, 3)
+        sigmoids(0, range(PACK))
+        bases(0, range(PACK))
+        sigmoids(1, early)
+        bases(1, early)
+        tanhs(0, range(PACK))
         cast_val(0)
-        cast_val(1)
         quantize_val(0, 0, PACK)
+        cast_val(1)
         cast_val(2)
-        cast_val(3)
         for t in range(PACK):
             quantize_val(1, t, t + 1)
-        scale_baseline(0, 0, HALF)
-        values(0)
-        sigmoids(1)
-        tanhs(1)
+        values(0, range(PACK))
+        scale_baseline(0)
+        sigmoids(1, late)
+        values(1, early)
+        tanhs(1, early)
+        bases(1, late)
+        tanhs(1, late)
         subtract(0)
-        nc.vector.tensor_copy(wq_bf[:].rearrange("p (c e) t -> p c t e", e=2), wq_raw[:].rearrange("p t (c e) -> p c t e", e=2))
-        values(1)
-        quantize_h(0)
+        values(1, late)
+        nc.scalar.copy(wq_bf[:].rearrange("p (c e) t -> p c t e", e=2), wq_raw[:].rearrange("p t (c e) -> p c t e", e=2))
+        scale_baseline_part(1, 0, 512)
         nc.vector.quantize_mx(out=wq_codes[:].bitcast(FP8X4), scales=wq_scales[:], in_=wq_bf[:].rearrange("p n t -> p (n t)"))
-        scale_baseline(1, 0, 256)
-        scale_baseline(1, 256, 256)
+        quantize_h(0)
         subtract(1)
-        finish(0, (0, 1), (nc.scalar.copy, nc.scalar.copy))
+        finish(0, (4, 5), (nc.scalar.copy, nc.scalar.copy))
         subtract(2)
         quantize_h(1)
-        finish(1, (2, 3), (nc.scalar.copy, nc.scalar.copy))
+        finish(1, (6, 7), (nc.scalar.copy, nc.scalar.copy))
+        subtract(3)
         quantize_h(2)
-        finish(2, (4, 5), (nc.scalar.copy, nc.vector.tensor_copy))
+        finish(2, (0, 1), (nc.scalar.copy, nc.scalar.copy))
+        quantize_h(3)
+        finish(3, (2, 3), (nc.scalar.copy, nc.vector.tensor_copy))

@@ -20,9 +20,8 @@ P = 128
 PACK = 4
 PASSES = K // (P * PACK)
 HALF = 512
-ROWS = 32
-GATE_COL = S
-BASE_COL = S + H
+ROWS = 16
+ROWS_AT = (48, 112)
 PLANE_W = S + 2 * H
 PIECE = 4 * PACK * H
 BASE_AT = PASSES * PIECE
@@ -46,14 +45,18 @@ def tile_list_replay_gated_q_kernel(tc, tab_words, tab_scales, offs, wval, wgate
         nc.sync.dma_start(offsets[:], offs)
 
         tab_rows = keep.tile([P, T], U8, name="tab_rows", align_bytes=64)
-        w_rows = keep.tile([ROWS, 2 * H], U8, name="w_rows", align_bytes=64)
-        planes = keep.tile([P, PASSES, PLANE_W], U8, name="planes", align_bytes=64)
-        nc.sync.dma_start(w_rows[0:ROWS, 0:H].bitcast(I32), wgate_scales.rearrange("a q c -> q a c").bitcast(I32))
-        nc.sync.dma_start(w_rows[0:ROWS, H:2 * H].bitcast(I32), wbase_scales.rearrange("a q c -> q a c").bitcast(I32))
-        nc.sync.dma_start(tab_rows[0:ROWS, :].bitcast(I32), tab_scales.rearrange("a q t -> q a t").bitcast(I32))
-        for lo, hi in ((32, 64), (64, 128)):
-            nc.vector.memset(tab_rows[lo:hi, :].bitcast(I32), 0)
-        nc.gpsimd.memset(planes[:].bitcast(I32), 0)
+        w_rows = keep.tile([P, 2 * H], U8, name="w_rows", align_bytes=64)
+        planes = [keep.tile([P, PLANE_W], U8, name="planes%d" % a, align_bytes=64) for a in range(PASSES)]
+        for a, scales in enumerate((wgate_scales, wbase_scales)):
+            nc.sync.dma_start(w_rows[ROWS_AT[a]:ROWS_AT[a] + ROWS, :].rearrange("q (a c) -> q a c", a=PASSES).bitcast(I32),
+                              scales.rearrange("a q c -> q a c").bitcast(I32))
+        for a in range(PASSES):
+            nc.sync.dma_start(tab_rows[ROWS_AT[a]:ROWS_AT[a] + ROWS, :].bitcast(I32), tab_scales[a].bitcast(I32))
+        for a in range(PASSES):
+            nc.vector.memset(tab_rows[64 * a:ROWS_AT[a], :].bitcast(I32), 0)
+            nc.gpsimd.memset(w_rows[64 * a:ROWS_AT[a], :].bitcast(I32), 0)
+        for a in range(PASSES):
+            nc.gpsimd.memset(planes[a][:].bitcast(I32), 0)
 
         gate_raw = keep.tile([P, PASSES, H // 2], I32, name="gate_raw")
         nc.sync.dma_start(gate_raw[:], wgate_words.rearrange("a p b -> p a b").bitcast(I32))
@@ -65,16 +68,21 @@ def tile_list_replay_gated_q_kernel(tc, tab_words, tab_scales, offs, wval, wgate
 
         load_table(0, keep.tile([P, T], I32, name="table0", align_bytes=64))
 
-        staged = keep.tile([ROWS, PLANE_W], U8, name="staged", align_bytes=64)
+        staged = keep.tile([P, PLANE_W], U8, name="staged", align_bytes=64)
         nc.vector.tensor_copy(staged[:, S:PLANE_W].bitcast(U16).rearrange("p (w t m) -> p w t m", w=2, t=PACK),
                               w_rows[:].bitcast(U16).rearrange("p (w m t) -> p w t m", w=2, t=PACK))
         picked_rows = reuse.tile([P, REUSED], U8, name="picked_rows", align_bytes=64, offset=0)
         nc.vector.tensor_copy(picked_rows[:, 0:S], tab_rows[:].indirect(offsets[:]))
-        nc.vector.tensor_copy(staged[:, 0:S].bitcast(I32), picked_rows[0:ROWS, 0:S].bitcast(I32))
-        for q in range(4):
-            nc.sync.dma_start(planes[32 * q:32 * q + 4].rearrange("p a c -> p (a c)").bitcast(I32),
-                              staged[8 * q:8 * q + 8, :].bitcast(I32))
+        nc.vector.tensor_copy(staged[:, 0:S].bitcast(I32), picked_rows[:, 0:S].bitcast(I32))
+
+        def move_planes(a):
+            for q in range(4):
+                nc.sync.dma_start(planes[a][32 * q:32 * q + 4, :].bitcast(I32),
+                                  staged[ROWS_AT[a] + 4 * q:ROWS_AT[a] + 4 * q + 4, :].bitcast(I32))
+
+        move_planes(0)
         load_table(1, reuse.tile([P, T], I32, name="table1", align_bytes=64, offset=TABLE_AT))
+        move_planes(1)
 
         gate_codes = keep.tile([P, PASSES, 2 * H], U8, name="gate_codes", align_bytes=64)
         nc.vector.tensor_copy(gate_codes[:].bitcast(I32).rearrange("p a (t m) -> p a m t", t=PACK),
@@ -104,18 +112,18 @@ def tile_list_replay_gated_q_kernel(tc, tab_words, tab_scales, offs, wval, wgate
         def product(acc, codes, scales, a, half, first=0):
             nc.tensor.matmul_mx(out=acc[:], lhsT=codes, lhsT_scale=scales,
                                 rhs=picked[a, half][:].bitcast(FP8X4),
-                                rhs_scale=planes[:, a, half * HALF:(half + 1) * HALF],
+                                rhs_scale=planes[a][:, half * HALF:(half + 1) * HALF],
                                 start=(a == first), stop=(a != first))
 
         def gate_pass(acc, a, t, half):
             product(acc, gate_codes[:, a, 2 * P * t:2 * P * (t + 1)].bitcast(FP4X4),
-                    planes[:, a, GATE_COL + P * t:GATE_COL + P * (t + 1)], a, half)
+                    planes[0][:, S + H * a + P * t:S + H * a + P * (t + 1)], a, half)
 
         base_codes = keep.tile([P, PASSES, H], I32, name="base_codes", align_bytes=64)
 
         def base_pass(acc, a, t, half):
             product(acc, base_codes[:, a, P * t:P * (t + 1)].bitcast(FP8X4),
-                    planes[:, a, BASE_COL + P * t:BASE_COL + P * (t + 1)], a, half)
+                    planes[1][:, S + H * a + P * t:S + H * a + P * (t + 1)], a, half)
 
         val_bf = [keep.tile([P, PACK, P, PACK], BF16, name="val_bf%d" % a, tag="val_bf%d" % a, align_bytes=64) for a in range(PASSES)]
         val_codes = [keep.tile([P, H], U32, name="val_codes%d" % a, align_bytes=64) for a in range(PASSES)]

@@ -20,8 +20,10 @@ P = 128
 PACK = 4
 PASSES = K // (P * PACK)
 HALF = 512
-ROWS = 16
-ROWS_AT = (48, 112)
+ROWS = 32
+ROWS_AT = P - ROWS
+GATE_COL = S
+BASE_COL = S + H
 PLANE_W = S + 2 * H
 PIECE = 4 * PACK * H
 BASE_AT = PASSES * PIECE
@@ -36,6 +38,7 @@ def tile_list_replay_gated_q_kernel(tc, tab_words, tab_scales, offs, wval, wgate
     with ExitStack() as ctx:
         keep = ctx.enter_context(tc.tile_pool(name="keep", bufs=1))
         reuse = ctx.enter_context(tc.tile_pool(name="reuse", bufs=1))
+        mixed = ctx.enter_context(tc.tile_pool(name="mixed", bufs=1))
         psum = ctx.enter_context(tc.psum_pool(name="psum", bufs=1))
 
         def bank(b):
@@ -46,17 +49,12 @@ def tile_list_replay_gated_q_kernel(tc, tab_words, tab_scales, offs, wval, wgate
 
         tab_rows = keep.tile([P, T], U8, name="tab_rows", align_bytes=64)
         w_rows = keep.tile([P, 2 * H], U8, name="w_rows", align_bytes=64)
-        planes = [keep.tile([P, PLANE_W], U8, name="planes%d" % a, align_bytes=64) for a in range(PASSES)]
-        for a, scales in enumerate((wgate_scales, wbase_scales)):
-            nc.sync.dma_start(w_rows[ROWS_AT[a]:ROWS_AT[a] + ROWS, :].rearrange("q (a c) -> q a c", a=PASSES).bitcast(I32),
-                              scales.rearrange("a q c -> q a c").bitcast(I32))
-        for a in range(PASSES):
-            nc.sync.dma_start(tab_rows[ROWS_AT[a]:ROWS_AT[a] + ROWS, :].bitcast(I32), tab_scales[a].bitcast(I32))
-        for a in range(PASSES):
-            nc.vector.memset(tab_rows[64 * a:ROWS_AT[a], :].bitcast(I32), 0)
-            nc.gpsimd.memset(w_rows[64 * a:ROWS_AT[a], :].bitcast(I32), 0)
-        for a in range(PASSES):
-            nc.gpsimd.memset(planes[a][:].bitcast(I32), 0)
+        planes = keep.tile([P, PASSES, PLANE_W], U8, name="planes", align_bytes=64)
+        nc.sync.dma_start(w_rows[ROWS_AT:P, 0:H].bitcast(I32), wgate_scales.rearrange("a q c -> q a c").bitcast(I32))
+        nc.sync.dma_start(w_rows[ROWS_AT:P, H:2 * H].bitcast(I32), wbase_scales.rearrange("a q c -> q a c").bitcast(I32))
+        nc.sync.dma_start(tab_rows[ROWS_AT:P, :].bitcast(I32), tab_scales.rearrange("a q t -> q a t").bitcast(I32))
+        nc.vector.memset(tab_rows[0:ROWS_AT, :].bitcast(I32), 0)
+        nc.gpsimd.memset(planes[:].bitcast(I32), 0)
 
         gate_raw = keep.tile([P, PASSES, H // 2], I32, name="gate_raw")
         nc.sync.dma_start(gate_raw[:], wgate_words.rearrange("a p b -> p a b").bitcast(I32))
@@ -69,20 +67,15 @@ def tile_list_replay_gated_q_kernel(tc, tab_words, tab_scales, offs, wval, wgate
         load_table(0, keep.tile([P, T], I32, name="table0", align_bytes=64))
 
         staged = keep.tile([P, PLANE_W], U8, name="staged", align_bytes=64)
-        nc.vector.tensor_copy(staged[:, S:PLANE_W].bitcast(U16).rearrange("p (w t m) -> p w t m", w=2, t=PACK),
-                              w_rows[:].bitcast(U16).rearrange("p (w m t) -> p w t m", w=2, t=PACK))
+        nc.vector.tensor_copy(staged[ROWS_AT:P, S:PLANE_W].bitcast(U16).rearrange("p (w t m) -> p w t m", w=2, t=PACK),
+                              w_rows[ROWS_AT:P, :].bitcast(U16).rearrange("p (w m t) -> p w t m", w=2, t=PACK))
         picked_rows = reuse.tile([P, REUSED], U8, name="picked_rows", align_bytes=64, offset=0)
         nc.vector.tensor_copy(picked_rows[:, 0:S], tab_rows[:].indirect(offsets[:]))
-        nc.vector.tensor_copy(staged[:, 0:S].bitcast(I32), picked_rows[:, 0:S].bitcast(I32))
-
-        def move_planes(a):
-            for q in range(4):
-                nc.sync.dma_start(planes[a][32 * q:32 * q + 4, :].bitcast(I32),
-                                  staged[ROWS_AT[a] + 4 * q:ROWS_AT[a] + 4 * q + 4, :].bitcast(I32))
-
-        move_planes(0)
+        nc.vector.tensor_copy(staged[ROWS_AT:P, 0:S].bitcast(I32), picked_rows[ROWS_AT:P, 0:S].bitcast(I32))
+        for q in (0, 2, 1, 3):
+            nc.sync.dma_start(planes[32 * q:32 * q + 4].rearrange("p a c -> p (a c)").bitcast(I32),
+                              staged[ROWS_AT + 8 * q:ROWS_AT + 8 * q + 8, :].bitcast(I32))
         load_table(1, reuse.tile([P, T], I32, name="table1", align_bytes=64, offset=TABLE_AT))
-        move_planes(1)
 
         gate_codes = keep.tile([P, PASSES, 2 * H], U8, name="gate_codes", align_bytes=64)
         nc.vector.tensor_copy(gate_codes[:].bitcast(I32).rearrange("p a (t m) -> p a m t", t=PACK),
@@ -112,18 +105,18 @@ def tile_list_replay_gated_q_kernel(tc, tab_words, tab_scales, offs, wval, wgate
         def product(acc, codes, scales, a, half, first=0):
             nc.tensor.matmul_mx(out=acc[:], lhsT=codes, lhsT_scale=scales,
                                 rhs=picked[a, half][:].bitcast(FP8X4),
-                                rhs_scale=planes[a][:, half * HALF:(half + 1) * HALF],
+                                rhs_scale=planes[:, a, half * HALF:(half + 1) * HALF],
                                 start=(a == first), stop=(a != first))
 
         def gate_pass(acc, a, t, half):
             product(acc, gate_codes[:, a, 2 * P * t:2 * P * (t + 1)].bitcast(FP4X4),
-                    planes[0][:, S + H * a + P * t:S + H * a + P * (t + 1)], a, half)
+                    planes[:, a, GATE_COL + P * t:GATE_COL + P * (t + 1)], a, half)
 
         base_codes = keep.tile([P, PASSES, H], I32, name="base_codes", align_bytes=64)
 
         def base_pass(acc, a, t, half):
             product(acc, base_codes[:, a, P * t:P * (t + 1)].bitcast(FP8X4),
-                    planes[1][:, S + H * a + P * t:S + H * a + P * (t + 1)], a, half)
+                    planes[:, a, BASE_COL + P * t:BASE_COL + P * (t + 1)], a, half)
 
         val_bf = [keep.tile([P, PACK, P, PACK], BF16, name="val_bf%d" % a, tag="val_bf%d" % a, align_bytes=64) for a in range(PASSES)]
         val_codes = [keep.tile([P, H], U32, name="val_codes%d" % a, align_bytes=64) for a in range(PASSES)]
@@ -143,11 +136,11 @@ def tile_list_replay_gated_q_kernel(tc, tab_words, tab_scales, offs, wval, wgate
             nc.vector.quantize_mx(out=val_codes[a][:, P * t0:P * t1].bitcast(FP8X4), scales=val_scales[a][:, P * t0:P * t1],
                                   in_=val_bf[a][:, t0:t1].rearrange("p t m j -> p (t m j)"))
 
-        sig = [keep.tile([P, PACK, HALF], F32, name="sig%d" % h) for h in range(2)]
+        sig = [keep.tile([P, PACK, HALF], F32, name="sig%d" % h, tag="sig%d" % h, align_bytes=64) for h in range(2)]
         squashed = [keep.tile([P, PACK, HALF], F32, name="squashed%d" % h) for h in range(2)]
         baseline = [keep.tile([P, PACK, HALF], F32, name="baseline0", tag="val_bf1", align_bytes=64),
                     keep.tile([P, PACK, HALF], F32, name="baseline1")]
-        gated = [keep.tile([P, PACK, HALF], F32, name="gated%d" % h) for h in range(2)]
+        gated = [keep.tile([P, PACK, HALF], F32, name="gated%d" % h, tag="gated%d" % h, align_bytes=64) for h in range(2)]
 
         gate_acc = {(half, t): bank(PACK * half + t) for half in range(2) for t in range(PACK)}
         for half in range(2):
@@ -171,9 +164,9 @@ def tile_list_replay_gated_q_kernel(tc, tab_words, tab_scales, offs, wval, wgate
 
         base_acc = {}
 
-        def bases(half, slices):
+        def bases(half, slices, first_bank):
             for t in slices:
-                base_acc[half, t] = bank(PACK * half + t)
+                base_acc[half, t] = bank(first_bank + t)
                 for a in range(PASSES):
                     base_pass(base_acc[half, t], a, t, half)
 
@@ -186,34 +179,38 @@ def tile_list_replay_gated_q_kernel(tc, tab_words, tab_scales, offs, wval, wgate
                 nc.gpsimd.tensor_scalar(baseline[half][:, t, :], squashed[half][:, t, :], gains[:, 2 * t:2 * t + 1], 0.0,
                                         ALU.mult, ALU.add)
 
-        def scale_baseline_part(half, lo, width):
-            for t in range(PACK):
+        def scale_baseline_part(half, slices, lo, width):
+            for t in slices:
                 nc.scalar.activation(baseline[half][:, t, lo:lo + width], squashed[half][:, t, lo:lo + width],
                                      ACT.Copy, scale=gains[:, 2 * t:2 * t + 1])
 
-        def values(half, slices):
+        def values(half, slices, first_bank=0):
             for t in slices:
-                acc = bank(t)
+                acc = bank(first_bank + t)
                 for a in (1, 0):
                     val_pass(acc, a, t, half, 1)
                 nc.vector.tensor_tensor(gated[half][:, t, :], acc[:], sig[half][:, t, :], ALU.mult)
 
         chunks = [(0, 512), (512, 256), (768, 128), (896, 128)]
-        h_mixed = [keep.tile([P, width, PACK], BF16, name="h_mixed%d" % i, align_bytes=64) for i, (c0, width) in enumerate(chunks)]
-        h_codes = [keep.tile([P, width], U32, name="h_codes%d" % i, align_bytes=64) for i, (c0, width) in enumerate(chunks)]
+        h_codes = [keep.tile([P, width], U32, name="h_codes%d" % i, tag="h_codes%d" % i if i else "gated0", align_bytes=64)
+                   for i, (c0, width) in enumerate(chunks)]
         h_scales = [keep.tile([P, width], U8, name="h_scales%d" % i, align_bytes=64) for i, (c0, width) in enumerate(chunks)]
+        h_mixed = {}
 
-        def subtract(i):
-            c0, width = chunks[i]
+        def subtract(c0, width, engine=nc.vector, at=None):
+            if at is None:
+                h_mixed[c0] = keep.tile([P, width, PACK], BF16, name="h_mixed%d" % c0, tag="sig1", align_bytes=64)
+            else:
+                h_mixed[c0] = mixed.tile([P, width, PACK], BF16, name="h_mixed%d" % c0, align_bytes=64, offset=at)
             half, lo = divmod(c0, HALF)
-            nc.vector.tensor_tensor(h_mixed[i][:].rearrange("p (c e) t -> p c t e", e=2),
-                                    gated[half][:, :, lo:lo + width].rearrange("p t (c e) -> p c t e", e=2),
-                                    baseline[half][:, :, lo:lo + width].rearrange("p t (c e) -> p c t e", e=2),
-                                    ALU.subtract)
+            engine.tensor_tensor(h_mixed[c0][:].rearrange("p (c e) t -> p c t e", e=2),
+                                 gated[half][:, :, lo:lo + width].rearrange("p t (c e) -> p c t e", e=2),
+                                 baseline[half][:, :, lo:lo + width].rearrange("p t (c e) -> p c t e", e=2),
+                                 ALU.subtract)
 
-        def quantize_h(i):
-            nc.vector.quantize_mx(out=h_codes[i][:].bitcast(FP8X4), scales=h_scales[i][:],
-                                  in_=h_mixed[i][:].rearrange("p c t -> p (c t)"))
+        def quantize_h(i, lo, width):
+            nc.vector.quantize_mx(out=h_codes[i][:, lo:lo + width].bitcast(FP8X4), scales=h_scales[i][:, lo:lo + width],
+                                  in_=h_mixed[chunks[i][0] + lo][:].rearrange("p c t -> p (c t)"))
 
         wq_bf = keep.tile([P, N, PACK], BF16, name="wq_bf", align_bytes=64)
         wq_codes = keep.tile([P, N], U32, name="wq_codes", align_bytes=64)
@@ -232,9 +229,9 @@ def tile_list_replay_gated_q_kernel(tc, tab_words, tab_scales, offs, wval, wgate
 
         early, late = (0, 1), (2, 3)
         sigmoids(0, range(PACK))
-        bases(0, range(PACK))
+        bases(0, range(PACK), 0)
         sigmoids(1, early)
-        bases(1, early)
+        bases(1, early, PACK)
         tanhs(0, range(PACK))
         cast_val(0)
         quantize_val(0, 0, PACK)
@@ -244,24 +241,28 @@ def tile_list_replay_gated_q_kernel(tc, tab_words, tab_scales, offs, wval, wgate
             quantize_val(1, t, t + 1)
         values(0, range(PACK))
         scale_baseline(0)
+        subtract(256, 256, nc.gpsimd, 1024)
         sigmoids(1, late)
         values(1, early)
+        values(1, late, PACK)
         tanhs(1, early)
-        bases(1, late)
-        tanhs(1, late)
-        subtract(0)
-        values(1, late)
+        bases(1, late, 0)
         nc.scalar.copy(wq_bf[:].rearrange("p (c e) t -> p c t e", e=2), wq_raw[:].rearrange("p t (c e) -> p c t e", e=2))
-        scale_baseline_part(1, 0, 512)
+        scale_baseline_part(1, early, 0, 256)
+        tanhs(1, late)
+        scale_baseline_part(1, late, 0, 256)
+        scale_baseline_part(1, range(PACK), 256, 256)
+        subtract(0, 256)
         nc.vector.quantize_mx(out=wq_codes[:].bitcast(FP8X4), scales=wq_scales[:], in_=wq_bf[:].rearrange("p n t -> p (n t)"))
-        quantize_h(0)
-        subtract(1)
+        quantize_h(0, 0, 256)
+        quantize_h(0, 256, 256)
+        subtract(512, 256, at=0)
         finish(0, (4, 5), (nc.scalar.copy, nc.scalar.copy))
-        subtract(2)
-        quantize_h(1)
+        subtract(768, 128, at=2048)
+        quantize_h(1, 0, 256)
         finish(1, (6, 7), (nc.scalar.copy, nc.scalar.copy))
-        subtract(3)
-        quantize_h(2)
+        subtract(896, 128, at=0)
+        quantize_h(2, 0, 128)
         finish(2, (0, 1), (nc.scalar.copy, nc.scalar.copy))
-        quantize_h(3)
+        quantize_h(3, 0, 128)
         finish(3, (2, 3), (nc.scalar.copy, nc.vector.tensor_copy))

@@ -21,7 +21,6 @@ PACK = 4
 PASSES = K // (P * PACK)
 HALF = 512
 ROWS = 32
-ROWS_AT = P - ROWS
 GATE_COL = S
 BASE_COL = S + H
 PLANE_W = S + 2 * H
@@ -38,7 +37,6 @@ def tile_list_replay_gated_q_kernel(tc, tab_words, tab_scales, offs, wval, wgate
     with ExitStack() as ctx:
         keep = ctx.enter_context(tc.tile_pool(name="keep", bufs=1))
         reuse = ctx.enter_context(tc.tile_pool(name="reuse", bufs=1))
-        mixed = ctx.enter_context(tc.tile_pool(name="mixed", bufs=1))
         psum = ctx.enter_context(tc.psum_pool(name="psum", bufs=1))
 
         def bank(b):
@@ -48,12 +46,13 @@ def tile_list_replay_gated_q_kernel(tc, tab_words, tab_scales, offs, wval, wgate
         nc.sync.dma_start(offsets[:], offs)
 
         tab_rows = keep.tile([P, T], U8, name="tab_rows", align_bytes=64)
-        w_rows = keep.tile([P, 2 * H], U8, name="w_rows", align_bytes=64)
+        w_rows = keep.tile([ROWS, 2 * H], U8, name="w_rows", align_bytes=64)
         planes = keep.tile([P, PASSES, PLANE_W], U8, name="planes", align_bytes=64)
-        nc.sync.dma_start(w_rows[ROWS_AT:P, 0:H].bitcast(I32), wgate_scales.rearrange("a q c -> q a c").bitcast(I32))
-        nc.sync.dma_start(w_rows[ROWS_AT:P, H:2 * H].bitcast(I32), wbase_scales.rearrange("a q c -> q a c").bitcast(I32))
-        nc.sync.dma_start(tab_rows[ROWS_AT:P, :].bitcast(I32), tab_scales.rearrange("a q t -> q a t").bitcast(I32))
-        nc.vector.memset(tab_rows[0:ROWS_AT, :].bitcast(I32), 0)
+        nc.sync.dma_start(w_rows[0:ROWS, 0:H].bitcast(I32), wgate_scales.rearrange("a q c -> q a c").bitcast(I32))
+        nc.sync.dma_start(w_rows[0:ROWS, H:2 * H].bitcast(I32), wbase_scales.rearrange("a q c -> q a c").bitcast(I32))
+        nc.sync.dma_start(tab_rows[0:ROWS, :].bitcast(I32), tab_scales.rearrange("a q t -> q a t").bitcast(I32))
+        for lo, hi in ((32, 64), (64, 128)):
+            nc.vector.memset(tab_rows[lo:hi, :].bitcast(I32), 0)
         nc.gpsimd.memset(planes[:].bitcast(I32), 0)
 
         gate_raw = keep.tile([P, PASSES, H // 2], I32, name="gate_raw")
@@ -66,15 +65,15 @@ def tile_list_replay_gated_q_kernel(tc, tab_words, tab_scales, offs, wval, wgate
 
         load_table(0, keep.tile([P, T], I32, name="table0", align_bytes=64))
 
-        staged = keep.tile([P, PLANE_W], U8, name="staged", align_bytes=64)
-        nc.vector.tensor_copy(staged[ROWS_AT:P, S:PLANE_W].bitcast(U16).rearrange("p (w t m) -> p w t m", w=2, t=PACK),
-                              w_rows[ROWS_AT:P, :].bitcast(U16).rearrange("p (w m t) -> p w t m", w=2, t=PACK))
+        staged = keep.tile([ROWS, PLANE_W], U8, name="staged", align_bytes=64)
+        nc.vector.tensor_copy(staged[:, S:PLANE_W].bitcast(U16).rearrange("p (w t m) -> p w t m", w=2, t=PACK),
+                              w_rows[:].bitcast(U16).rearrange("p (w m t) -> p w t m", w=2, t=PACK))
         picked_rows = reuse.tile([P, REUSED], U8, name="picked_rows", align_bytes=64, offset=0)
         nc.vector.tensor_copy(picked_rows[:, 0:S], tab_rows[:].indirect(offsets[:]))
-        nc.vector.tensor_copy(staged[ROWS_AT:P, 0:S].bitcast(I32), picked_rows[ROWS_AT:P, 0:S].bitcast(I32))
-        for q in (0, 2, 1, 3):
+        nc.vector.tensor_copy(staged[:, 0:S].bitcast(I32), picked_rows[0:ROWS, 0:S].bitcast(I32))
+        for q in range(4):
             nc.sync.dma_start(planes[32 * q:32 * q + 4].rearrange("p a c -> p (a c)").bitcast(I32),
-                              staged[ROWS_AT + 8 * q:ROWS_AT + 8 * q + 8, :].bitcast(I32))
+                              staged[8 * q:8 * q + 8, :].bitcast(I32))
         load_table(1, reuse.tile([P, T], I32, name="table1", align_bytes=64, offset=TABLE_AT))
 
         gate_codes = keep.tile([P, PASSES, 2 * H], U8, name="gate_codes", align_bytes=64)
@@ -174,8 +173,8 @@ def tile_list_replay_gated_q_kernel(tc, tab_words, tab_scales, offs, wval, wgate
             for t in slices:
                 nc.scalar.activation(squashed[half][:, t, :], base_acc[half, t][:], ACT.Tanh)
 
-        def scale_baseline(half):
-            for t in range(PACK):
+        def scale_baseline(half, slices):
+            for t in slices:
                 nc.gpsimd.tensor_scalar(baseline[half][:, t, :], squashed[half][:, t, :], gains[:, 2 * t:2 * t + 1], 0.0,
                                         ALU.mult, ALU.add)
 
@@ -187,30 +186,27 @@ def tile_list_replay_gated_q_kernel(tc, tab_words, tab_scales, offs, wval, wgate
         def values(half, slices, first_bank=0):
             for t in slices:
                 acc = bank(first_bank + t)
-                for a in (1, 0):
-                    val_pass(acc, a, t, half, 1)
+                first = 0 if (half, t) == (0, 0) else 1
+                for a in (first, 1 - first):
+                    val_pass(acc, a, t, half, first)
                 nc.vector.tensor_tensor(gated[half][:, t, :], acc[:], sig[half][:, t, :], ALU.mult)
 
         chunks = [(0, 512), (512, 256), (768, 128), (896, 128)]
-        h_codes = [keep.tile([P, width], U32, name="h_codes%d" % i, tag="h_codes%d" % i if i else "gated0", align_bytes=64)
+        h_mixed = [keep.tile([P, width, PACK], BF16, name="h_mixed%d" % i, align_bytes=64)
                    for i, (c0, width) in enumerate(chunks)]
+        h_codes = [keep.tile([P, width], U32, name="h_codes%d" % i, align_bytes=64) for i, (c0, width) in enumerate(chunks)]
         h_scales = [keep.tile([P, width], U8, name="h_scales%d" % i, align_bytes=64) for i, (c0, width) in enumerate(chunks)]
-        h_mixed = {}
 
-        def subtract(c0, width, engine=nc.vector, at=None):
-            if at is None:
-                h_mixed[c0] = keep.tile([P, width, PACK], BF16, name="h_mixed%d" % c0, tag="sig1", align_bytes=64)
-            else:
-                h_mixed[c0] = mixed.tile([P, width, PACK], BF16, name="h_mixed%d" % c0, align_bytes=64, offset=at)
-            half, lo = divmod(c0, HALF)
-            engine.tensor_tensor(h_mixed[c0][:].rearrange("p (c e) t -> p c t e", e=2),
-                                 gated[half][:, :, lo:lo + width].rearrange("p t (c e) -> p c t e", e=2),
-                                 baseline[half][:, :, lo:lo + width].rearrange("p t (c e) -> p c t e", e=2),
-                                 ALU.subtract)
+        def subtract(i, width):
+            half, lo = divmod(chunks[i][0], HALF)
+            nc.vector.tensor_tensor(h_mixed[i][:, 0:width].rearrange("p (c e) t -> p c t e", e=2),
+                                    gated[half][:, :, lo:lo + width].rearrange("p t (c e) -> p c t e", e=2),
+                                    baseline[half][:, :, lo:lo + width].rearrange("p t (c e) -> p c t e", e=2),
+                                    ALU.subtract)
 
-        def quantize_h(i, lo, width):
-            nc.vector.quantize_mx(out=h_codes[i][:, lo:lo + width].bitcast(FP8X4), scales=h_scales[i][:, lo:lo + width],
-                                  in_=h_mixed[chunks[i][0] + lo][:].rearrange("p c t -> p (c t)"))
+        def quantize_h(i):
+            nc.vector.quantize_mx(out=h_codes[i][:].bitcast(FP8X4), scales=h_scales[i][:],
+                                  in_=h_mixed[i][:].rearrange("p c t -> p (c t)"))
 
         wq_bf = keep.tile([P, N, PACK], BF16, name="wq_bf", align_bytes=64)
         wq_codes = keep.tile([P, N], U32, name="wq_codes", align_bytes=64)
@@ -225,9 +221,12 @@ def tile_list_replay_gated_q_kernel(tc, tab_words, tab_scales, offs, wval, wgate
                                     lhsT_scale=wq_scales[:, P * nt:P * (nt + 1)],
                                     rhs=h_codes[i][:].bitcast(FP8X4), rhs_scale=h_scales[i][:], start=True, stop=True)
                 copies[nt](result[:, nt, :], acc[:, 0:width])
-            nc.sync.dma_start(out[:, c0:c0 + width].rearrange("(u p) c -> p u c", p=P), result[:])
+                if i == 0:
+                    nc.sync.dma_start(out[P * nt:P * (nt + 1), c0:c0 + width], result[:, nt, :])
+            if i > 0:
+                nc.sync.dma_start(out[:, c0:c0 + width].rearrange("(u p) c -> p u c", p=P), result[:])
 
-        early, late = (0, 1), (2, 3)
+        early, late = (0,), (1, 2, 3)
         sigmoids(0, range(PACK))
         bases(0, range(PACK), 0)
         sigmoids(1, early)
@@ -240,29 +239,27 @@ def tile_list_replay_gated_q_kernel(tc, tab_words, tab_scales, offs, wval, wgate
         for t in range(PACK):
             quantize_val(1, t, t + 1)
         values(0, range(PACK))
-        scale_baseline(0)
-        subtract(256, 256, nc.gpsimd, 1024)
+        scale_baseline(0, (0, 1, 2))
         sigmoids(1, late)
-        values(1, early)
-        values(1, late, PACK)
+        scale_baseline_part(0, (3,), 0, HALF)
+        values(1, (0,))
+        values(1, (1,), PACK)
         tanhs(1, early)
         bases(1, late, 0)
         nc.scalar.copy(wq_bf[:].rearrange("p (c e) t -> p c t e", e=2), wq_raw[:].rearrange("p t (c e) -> p c t e", e=2))
-        scale_baseline_part(1, early, 0, 256)
         tanhs(1, late)
-        scale_baseline_part(1, late, 0, 256)
-        scale_baseline_part(1, range(PACK), 256, 256)
-        subtract(0, 256)
+        subtract(0, HALF)
         nc.vector.quantize_mx(out=wq_codes[:].bitcast(FP8X4), scales=wq_scales[:], in_=wq_bf[:].rearrange("p n t -> p (n t)"))
-        quantize_h(0, 0, 256)
-        quantize_h(0, 256, 256)
-        subtract(512, 256, at=0)
-        finish(0, (4, 5), (nc.scalar.copy, nc.scalar.copy))
-        subtract(768, 128, at=2048)
-        quantize_h(1, 0, 256)
-        finish(1, (6, 7), (nc.scalar.copy, nc.scalar.copy))
-        subtract(896, 128, at=0)
-        quantize_h(2, 0, 128)
-        finish(2, (0, 1), (nc.scalar.copy, nc.scalar.copy))
-        quantize_h(3, 0, 128)
+        values(1, (2, 3), PACK)
+        scale_baseline_part(1, range(PACK), 0, HALF)
+        quantize_h(0)
+        subtract(1, 256)
+        finish(0, (4, 0), (nc.scalar.copy, nc.scalar.copy))
+        subtract(2, 128)
+        quantize_h(1)
+        finish(1, (5, 6), (nc.scalar.copy, nc.scalar.copy))
+        subtract(3, 128)
+        quantize_h(2)
+        finish(2, (7, 1), (nc.scalar.copy, nc.scalar.copy))
+        quantize_h(3)
         finish(3, (2, 3), (nc.scalar.copy, nc.vector.tensor_copy))

@@ -20,6 +20,7 @@ P = 128
 PACK = 4
 PASSES = K // (P * PACK)
 HALF = 512
+LAST = 160
 ROWS = 32
 GATE_COL = S
 BASE_COL = S + H
@@ -71,7 +72,7 @@ def tile_list_replay_gated_q_kernel(tc, tab_words, tab_scales, offs, wval, wgate
         picked_rows = reuse.tile([P, REUSED], U8, name="picked_rows", align_bytes=64, offset=0)
         nc.vector.tensor_copy(picked_rows[:, 0:S], tab_rows[:].indirect(offsets[:]))
         nc.vector.tensor_copy(staged[:, 0:S].bitcast(I32), picked_rows[0:ROWS, 0:S].bitcast(I32))
-        for q in range(4):
+        for q in (0, 2, 1, 3):
             nc.sync.dma_start(planes[32 * q:32 * q + 4].rearrange("p a c -> p (a c)").bitcast(I32),
                               staged[8 * q:8 * q + 8, :].bitcast(I32))
         load_table(1, reuse.tile([P, T], I32, name="table1", align_bytes=64, offset=TABLE_AT))
@@ -84,7 +85,7 @@ def tile_list_replay_gated_q_kernel(tc, tab_words, tab_scales, offs, wval, wgate
         nc.sync.dma_start(base_raw[:].rearrange("p (a c) -> p a c", a=PASSES),
                           wbase_words.rearrange("a p c i -> p a (c i)").bitcast(I32))
         gains = reuse.tile([P, 8], F32, name="gains", align_bytes=64, offset=GAINS_AT)
-        val_pieces = [(0, 0, H), (1, 0, H // 2), (1, H // 2, H // 2)]
+        val_pieces = [(0, 0, H), (1, 0, H - LAST), (1, H - LAST, LAST)]
         val_raw = []
         for i, (a, c0, width) in enumerate(val_pieces):
             piece = reuse.tile([P, PACK, width], F32, name="piece%d" % i, align_bytes=64, offset=a * PIECE + 16 * c0)
@@ -125,11 +126,11 @@ def tile_list_replay_gated_q_kernel(tc, tab_words, tab_scales, offs, wval, wgate
             product(acc, val_codes[a][:, P * t:P * (t + 1)].bitcast(FP8X4), val_scales[a][:, P * t:P * (t + 1)], a, half,
                     first)
 
-        def cast_val(i):
+        def cast_val(i, t0=0, t1=PACK):
             a, c0, width = val_pieces[i]
             m0, m1 = c0 // PACK, (c0 + width) // PACK
-            nc.vector.tensor_copy(val_bf[a][:, :, m0:m1, :].rearrange("p t (m e) j -> p m t j e", e=2),
-                                  val_raw[i][:].rearrange("p j (m t e) -> p m t j e", t=PACK, e=2))
+            nc.vector.tensor_copy(val_bf[a][:, t0:t1, m0:m1, :].rearrange("p t (m e) j -> p m t j e", e=2),
+                                  val_raw[i][:].rearrange("p j (m t e) -> p m t j e", t=PACK, e=2)[:, :, t0:t1])
 
         def quantize_val(a, t0, t1):
             nc.vector.quantize_mx(out=val_codes[a][:, P * t0:P * t1].bitcast(FP8X4), scales=val_scales[a][:, P * t0:P * t1],
@@ -235,7 +236,8 @@ def tile_list_replay_gated_q_kernel(tc, tab_words, tab_scales, offs, wval, wgate
         cast_val(0)
         quantize_val(0, 0, PACK)
         cast_val(1)
-        cast_val(2)
+        cast_val(2, 0, 2)
+        cast_val(2, 2, PACK)
         for t in range(PACK):
             quantize_val(1, t, t + 1)
         values(0, range(PACK))
@@ -249,10 +251,12 @@ def tile_list_replay_gated_q_kernel(tc, tab_words, tab_scales, offs, wval, wgate
         nc.scalar.copy(wq_bf[:].rearrange("p (c e) t -> p c t e", e=2), wq_raw[:].rearrange("p t (c e) -> p c t e", e=2))
         tanhs(1, late)
         subtract(0, HALF)
-        nc.vector.quantize_mx(out=wq_codes[:].bitcast(FP8X4), scales=wq_scales[:], in_=wq_bf[:].rearrange("p n t -> p (n t)"))
-        values(1, (2, 3), PACK)
-        scale_baseline_part(1, range(PACK), 0, HALF)
+        values(1, (2,), PACK)
         quantize_h(0)
+        values(1, (3,), PACK)
+        for lo in (0, HALF // 2):
+            scale_baseline_part(1, range(PACK), lo, HALF // 2)
+        nc.vector.quantize_mx(out=wq_codes[:].bitcast(FP8X4), scales=wq_scales[:], in_=wq_bf[:].rearrange("p n t -> p (n t)"))
         subtract(1, 256)
         finish(0, (4, 0), (nc.scalar.copy, nc.scalar.copy))
         subtract(2, 128)

@@ -245,18 +245,17 @@ def tile_list_replay_gated_q_kernel(tc, tab_words, tab_scales, offs, wval, wgate
         sigmoids(1, late)
         scale_baseline_part(0, (3,), 0, HALF)
         values(1, (0,))
-        values(1, (1,), PACK)
+        values(1, (1, 2), PACK)
         tanhs(1, early)
         bases(1, late, 0)
         nc.scalar.copy(wq_bf[:].rearrange("p (c e) t -> p c t e", e=2), wq_raw[:].rearrange("p t (c e) -> p c t e", e=2))
         tanhs(1, late)
         subtract(0, HALF)
-        values(1, (2,), PACK)
-        quantize_h(0)
+        nc.vector.quantize_mx(out=wq_codes[:].bitcast(FP8X4), scales=wq_scales[:], in_=wq_bf[:].rearrange("p n t -> p (n t)"))
         values(1, (3,), PACK)
         for lo in (0, HALF // 2):
             scale_baseline_part(1, range(PACK), lo, HALF // 2)
-        nc.vector.quantize_mx(out=wq_codes[:].bitcast(FP8X4), scales=wq_scales[:], in_=wq_bf[:].rearrange("p n t -> p (n t)"))
+        quantize_h(0)
         subtract(1, 256)
         finish(0, (4, 0), (nc.scalar.copy, nc.scalar.copy))
         subtract(2, 128)

@@ -21,7 +21,7 @@ PACK = 4
 PASSES = K // (P * PACK)
 HALF = 512
 LAST = 160
-ROWS = 32
+ROW0 = P - 32
 GATE_COL = S
 BASE_COL = S + H
 PLANE_W = S + 2 * H
@@ -44,16 +44,14 @@ def tile_list_replay_gated_q_kernel(tc, tab_words, tab_scales, offs, wval, wgate
             return psum.tile([P, HALF], F32, name="bank%d" % b, tag="bank%d" % b)
 
         offsets = keep.tile([P, S // 16], U16, name="offsets")
-        nc.sync.dma_start(offsets[:], offs)
-
         tab_rows = keep.tile([P, T], U8, name="tab_rows", align_bytes=64)
-        w_rows = keep.tile([ROWS, 2 * H], U8, name="w_rows", align_bytes=64)
+        w_rows = [keep.tile([P, H], U8, name="w_rows%d" % w, align_bytes=64) for w in range(2)]
         planes = keep.tile([P, PASSES, PLANE_W], U8, name="planes", align_bytes=64)
-        nc.sync.dma_start(w_rows[0:ROWS, 0:H].bitcast(I32), wgate_scales.rearrange("a q c -> q a c").bitcast(I32))
-        nc.sync.dma_start(w_rows[0:ROWS, H:2 * H].bitcast(I32), wbase_scales.rearrange("a q c -> q a c").bitcast(I32))
-        nc.sync.dma_start(tab_rows[0:ROWS, :].bitcast(I32), tab_scales.rearrange("a q t -> q a t").bitcast(I32))
-        for lo, hi in ((32, 64), (64, 128)):
-            nc.vector.memset(tab_rows[lo:hi, :].bitcast(I32), 0)
+        nc.sync.dma_start(w_rows[0][ROW0:P].bitcast(I32), wgate_scales.rearrange("a q c -> q a c").bitcast(I32))
+        nc.sync.dma_start(tab_rows[ROW0:P, :].bitcast(I32), tab_scales.rearrange("a q t -> q a t").bitcast(I32))
+        nc.sync.dma_start(w_rows[1][ROW0:P].bitcast(I32), wbase_scales.rearrange("a q c -> q a c").bitcast(I32))
+        nc.sync.dma_start(offsets[:], offs)
+        nc.vector.memset(tab_rows[0:ROW0, :].bitcast(I32), 0)
         nc.gpsimd.memset(planes[:].bitcast(I32), 0)
 
         gate_raw = keep.tile([P, PASSES, H // 2], I32, name="gate_raw")
@@ -66,15 +64,16 @@ def tile_list_replay_gated_q_kernel(tc, tab_words, tab_scales, offs, wval, wgate
 
         load_table(0, keep.tile([P, T], I32, name="table0", align_bytes=64))
 
-        staged = keep.tile([ROWS, PLANE_W], U8, name="staged", align_bytes=64)
-        nc.vector.tensor_copy(staged[:, S:PLANE_W].bitcast(U16).rearrange("p (w t m) -> p w t m", w=2, t=PACK),
-                              w_rows[:].bitcast(U16).rearrange("p (w m t) -> p w t m", w=2, t=PACK))
+        staged = keep.tile([P, PLANE_W], U8, name="staged", align_bytes=64)
+        for w in range(2):
+            nc.scalar.copy(staged[ROW0:P, S + H * w:S + H * (w + 1)].bitcast(U16).rearrange("p (t m) -> p t m", t=PACK),
+                           w_rows[w][ROW0:P].bitcast(U16).rearrange("p (m t) -> p t m", t=PACK))
         picked_rows = reuse.tile([P, REUSED], U8, name="picked_rows", align_bytes=64, offset=0)
         nc.vector.tensor_copy(picked_rows[:, 0:S], tab_rows[:].indirect(offsets[:]))
-        nc.vector.tensor_copy(staged[:, 0:S].bitcast(I32), picked_rows[0:ROWS, 0:S].bitcast(I32))
+        nc.vector.tensor_copy(staged[ROW0:P, 0:S].bitcast(I32), picked_rows[ROW0:P, 0:S].bitcast(I32))
         for q in (0, 2, 1, 3):
             nc.sync.dma_start(planes[32 * q:32 * q + 4].rearrange("p a c -> p (a c)").bitcast(I32),
-                              staged[8 * q:8 * q + 8, :].bitcast(I32))
+                              staged[ROW0 + 8 * q:ROW0 + 8 * q + 8, :].bitcast(I32))
         load_table(1, reuse.tile([P, T], I32, name="table1", align_bytes=64, offset=TABLE_AT))
 
         gate_codes = keep.tile([P, PASSES, 2 * H], U8, name="gate_codes", align_bytes=64)

@@ -47,10 +47,10 @@ def tile_list_replay_gated_q_kernel(tc, tab_words, tab_scales, offs, wval, wgate
         tab_rows = keep.tile([P, T], U8, name="tab_rows", align_bytes=64)
         w_rows = [keep.tile([P, H], U8, name="w_rows%d" % w, align_bytes=64) for w in range(2)]
         planes = keep.tile([P, PASSES, PLANE_W], U8, name="planes", align_bytes=64)
-        nc.sync.dma_start(w_rows[0][ROW0:P].bitcast(I32), wgate_scales.rearrange("a q c -> q a c").bitcast(I32))
         nc.sync.dma_start(tab_rows[ROW0:P, :].bitcast(I32), tab_scales.rearrange("a q t -> q a t").bitcast(I32))
-        nc.sync.dma_start(w_rows[1][ROW0:P].bitcast(I32), wbase_scales.rearrange("a q c -> q a c").bitcast(I32))
         nc.sync.dma_start(offsets[:], offs)
+        nc.scalar.dma_start(w_rows[0][ROW0:P].bitcast(I32), wgate_scales.rearrange("a q c -> q a c").bitcast(I32))
+        nc.scalar.dma_start(w_rows[1][ROW0:P].bitcast(I32), wbase_scales.rearrange("a q c -> q a c").bitcast(I32))
         nc.vector.memset(tab_rows[0:ROW0, :].bitcast(I32), 0)
         nc.gpsimd.memset(planes[:].bitcast(I32), 0)
 

@@ -191,7 +191,7 @@ def tile_list_replay_gated_q_kernel(tc, tab_words, tab_scales, offs, wval, wgate
                     val_pass(acc, a, t, half, first)
                 nc.vector.tensor_tensor(gated[half][:, t, :], acc[:], sig[half][:, t, :], ALU.mult)
 
-        chunks = [(0, 512), (512, 256), (768, 128), (896, 128)]
+        chunks = [(0, 512), (512, 128), (640, 128), (768, 128), (896, 128)]
         h_mixed = [keep.tile([P, width, PACK], BF16, name="h_mixed%d" % i, align_bytes=64)
                    for i, (c0, width) in enumerate(chunks)]
         h_codes = [keep.tile([P, width], U32, name="h_codes%d" % i, align_bytes=64) for i, (c0, width) in enumerate(chunks)]
@@ -212,9 +212,14 @@ def tile_list_replay_gated_q_kernel(tc, tab_words, tab_scales, offs, wval, wgate
         wq_codes = keep.tile([P, N], U32, name="wq_codes", align_bytes=64)
         wq_scales = keep.tile([P, N], U8, name="wq_scales", align_bytes=64)
 
+        pair = keep.tile([P, N // P, 256], F32, name="pair")
+
         def finish(i, banks, copies):
             c0, width = chunks[i]
-            result = keep.tile([P, N // P, width], F32, name="result%d" % i)
+            if i not in (1, 2):
+                result = keep.tile([P, N // P, width], F32, name="result%d" % i)
+            else:
+                result = pair[:, :, c0 - HALF:c0 - HALF + width]
             for nt in range(N // P):
                 acc = bank(banks[nt])
                 nc.tensor.matmul_mx(out=acc[:, 0:width], lhsT=wq_codes[:, P * nt:P * (nt + 1)].bitcast(FP8X4),
@@ -223,8 +228,10 @@ def tile_list_replay_gated_q_kernel(tc, tab_words, tab_scales, offs, wval, wgate
                 copies[nt](result[:, nt, :], acc[:, 0:width])
                 if i == 0:
                     nc.sync.dma_start(out[P * nt:P * (nt + 1), c0:c0 + width], result[:, nt, :])
-            if i > 0:
+            if i > 2:
                 nc.sync.dma_start(out[:, c0:c0 + width].rearrange("(u p) c -> p u c", p=P), result[:])
+            if i == 2:
+                nc.sync.dma_start(out[:, HALF:HALF + 256].rearrange("(u p) c -> p u c", p=P), pair[:])
 
         early, late = (0,), (1, 2, 3)
         sigmoids(0, range(PACK))
@@ -255,7 +262,7 @@ def tile_list_replay_gated_q_kernel(tc, tab_words, tab_scales, offs, wval, wgate
         for lo in (0, HALF // 2):
             scale_baseline_part(1, range(PACK), lo, HALF // 2)
         quantize_h(0)
-        subtract(1, 256)
+        subtract(1, 128)
         finish(0, (4, 0), (nc.scalar.copy, nc.scalar.copy))
         subtract(2, 128)
         quantize_h(1)
@@ -263,5 +270,8 @@ def tile_list_replay_gated_q_kernel(tc, tab_words, tab_scales, offs, wval, wgate
         subtract(3, 128)
         quantize_h(2)
         finish(2, (7, 1), (nc.scalar.copy, nc.scalar.copy))
+        subtract(4, 128)
         quantize_h(3)
-        finish(3, (2, 3), (nc.scalar.copy, nc.vector.tensor_copy))
+        finish(3, (2, 3), (nc.scalar.copy, nc.scalar.copy))
+        quantize_h(4)
+        finish(4, (4, 5), (nc.scalar.copy, nc.vector.tensor_copy))

from contextlib import ExitStack

import concourse.mybir as mybir

K, T, S, H, N = 1024, 4096, 1024, 512, 256
FLOPS = 2 * S * H * (3 * K + N)

F32 = mybir.dt.float32
BF16 = mybir.dt.bfloat16
I32 = mybir.dt.int32
U32 = mybir.dt.uint32
U16 = mybir.dt.uint16
U8 = mybir.dt.uint8
FP8X4 = mybir.dt.float8_e4m3fn_x4
FP4X4 = mybir.dt.float4_e2m1fn_x4
ACT = mybir.ActivationFunctionType
ALU = mybir.AluOpType

P = 128
PACK = 4
PASSES = K // (P * PACK)
HALF = 512
LAST = 160
ROW0 = P - 32
GATE_COL = S
BASE_COL = S + H
PLANE_W = S + 2 * H
PIECE = 4 * PACK * H
BASE_AT = PASSES * PIECE
GAINS_AT = BASE_AT + 4 * PASSES * H
TABLE_AT = GAINS_AT + 64
REUSED = TABLE_AT + 4 * T


def tile_list_replay_gated_q_kernel(tc, tab_words, tab_scales, offs, wval, wgate_words, wgate_scales,
                                             wbase_words, wbase_scales, gain, wq, out):
    nc = tc.nc
    with ExitStack() as ctx:
        keep = ctx.enter_context(tc.tile_pool(name="keep", bufs=1))
        reuse = ctx.enter_context(tc.tile_pool(name="reuse", bufs=1))
        psum = ctx.enter_context(tc.psum_pool(name="psum", bufs=1))

        def bank(b):
            return psum.tile([P, HALF], F32, name="bank%d" % b, tag="bank%d" % b)

        offsets = keep.tile([P, S // 16], U16, name="offsets")
        tab_rows = keep.tile([P, T], U8, name="tab_rows", align_bytes=64)
        w_rows = [keep.tile([P, H], U8, name="w_rows%d" % w, align_bytes=64) for w in range(2)]
        planes = keep.tile([P, PASSES, PLANE_W], U8, name="planes", align_bytes=64)
        nc.sync.dma_start(tab_rows[ROW0:P, :].bitcast(I32), tab_scales.rearrange("a q t -> q a t").bitcast(I32))
        nc.sync.dma_start(offsets[:], offs)
        nc.scalar.dma_start(w_rows[0][ROW0:P].bitcast(I32), wgate_scales.rearrange("a q c -> q a c").bitcast(I32))
        nc.scalar.dma_start(w_rows[1][ROW0:P].bitcast(I32), wbase_scales.rearrange("a q c -> q a c").bitcast(I32))
        nc.vector.memset(tab_rows[0:ROW0, :].bitcast(I32), 0)
        nc.gpsimd.memset(planes[:].bitcast(I32), 0)

        gate_raw = keep.tile([P, PASSES, H // 2], I32, name="gate_raw")
        nc.sync.dma_start(gate_raw[:], wgate_words.rearrange("a p b -> p a b").bitcast(I32))
        tables = []

        def load_table(a, table):
            nc.sync.dma_start(table[:], tab_words[a].rearrange("p t i -> p (t i)").bitcast(I32))
            tables.append(table)

        load_table(0, keep.tile([P, T], I32, name="table0", align_bytes=64))

        staged = keep.tile([P, PLANE_W], U8, name="staged", align_bytes=64)
        for w in range(2):
            nc.scalar.copy(staged[ROW0:P, S + H * w:S + H * (w + 1)].bitcast(U16).rearrange("p (t m) -> p t m", t=PACK),
                           w_rows[w][ROW0:P].bitcast(U16).rearrange("p (m t) -> p t m", t=PACK))
        picked_rows = reuse.tile([P, REUSED], U8, name="picked_rows", align_bytes=64, offset=0)
        nc.vector.tensor_copy(picked_rows[:, 0:S], tab_rows[:].indirect(offsets[:]))
        nc.vector.tensor_copy(staged[ROW0:P, 0:S].bitcast(I32), picked_rows[ROW0:P, 0:S].bitcast(I32))
        for q in (0, 2, 1, 3):
            nc.sync.dma_start(planes[32 * q:32 * q + 4].rearrange("p a c -> p (a c)").bitcast(I32),
                              staged[ROW0 + 8 * q:ROW0 + 8 * q + 8, :].bitcast(I32))
        load_table(1, reuse.tile([P, T], I32, name="table1", align_bytes=64, offset=TABLE_AT))

        gate_codes = keep.tile([P, PASSES, 2 * H], U8, name="gate_codes", align_bytes=64)
        nc.vector.tensor_copy(gate_codes[:].bitcast(I32).rearrange("p a (t m) -> p a m t", t=PACK),
                              gate_raw[:].rearrange("p a (m t) -> p a m t", t=PACK))

        base_raw = reuse.tile([P, PASSES * H], I32, name="base_raw", align_bytes=64, offset=BASE_AT)
        nc.sync.dma_start(base_raw[:].rearrange("p (a c) -> p a c", a=PASSES),
                          wbase_words.rearrange("a p c i -> p a (c i)").bitcast(I32))
        gains = reuse.tile([P, 8], F32, name="gains", align_bytes=64, offset=GAINS_AT)
        val_pieces = [(0, 0, H), (1, 0, H - LAST), (1, H - LAST, LAST)]
        val_raw = []
        for i, (a, c0, width) in enumerate(val_pieces):
            piece = reuse.tile([P, PACK, width], F32, name="piece%d" % i, align_bytes=64, offset=a * PIECE + 16 * c0)
            nc.sync.dma_start(piece[:], wval[a * 512:(a + 1) * 512, c0:c0 + width].rearrange("(p j) c -> p j c", j=PACK))
            val_raw.append(piece)
        for e in range(2):
            nc.sync.dma_start(gains[e:P:2, 0:7], gain.rearrange("(m x) -> m x", x=8)[:, e:e + 7])

        picked = {}

        def gather(a, half):
            words = keep.tile([P, HALF], U32, name="picked%d%d" % (a, half), align_bytes=64)
            cols = HALF // 16
            nc.vector.tensor_copy(words[:], tables[a][:].bitcast(U32).indirect(offsets[:, half * cols:(half + 1) * cols]))
            picked[a, half] = words

        def product(acc, codes, scales, a, half, first=0):
            nc.tensor.matmul_mx(out=acc[:], lhsT=codes, lhsT_scale=scales,
                                rhs=picked[a, half][:].bitcast(FP8X4),
                                rhs_scale=planes[:, a, half * HALF:(half + 1) * HALF],
                                start=(a == first), stop=(a != first))

        def gate_pass(acc, a, t, half):
            product(acc, gate_codes[:, a, 2 * P * t:2 * P * (t + 1)].bitcast(FP4X4),
                    planes[:, a, GATE_COL + P * t:GATE_COL + P * (t + 1)], a, half)

        base_codes = keep.tile([P, PASSES, H], I32, name="base_codes", align_bytes=64)

        def base_pass(acc, a, t, half):
            product(acc, base_codes[:, a, P * t:P * (t + 1)].bitcast(FP8X4),
                    planes[:, a, BASE_COL + P * t:BASE_COL + P * (t + 1)], a, half)

        val_bf = [keep.tile([P, PACK, P, PACK], BF16, name="val_bf%d" % a, tag="val_bf%d" % a, align_bytes=64) for a in range(PASSES)]
        val_codes = [keep.tile([P, H], U32, name="val_codes%d" % a, align_bytes=64) for a in range(PASSES)]
        val_scales = [keep.tile([P, H], U8, name="val_scales%d" % a, align_bytes=64) for a in range(PASSES)]

        def val_pass(acc, a, t, half, first):
            product(acc, val_codes[a][:, P * t:P * (t + 1)].bitcast(FP8X4), val_scales[a][:, P * t:P * (t + 1)], a, half,
                    first)

        def cast_val(i, t0=0, t1=PACK):
            a, c0, width = val_pieces[i]
            m0, m1 = c0 // PACK, (c0 + width) // PACK
            nc.vector.tensor_copy(val_bf[a][:, t0:t1, m0:m1, :].rearrange("p t (m e) j -> p m t j e", e=2),
                                  val_raw[i][:].rearrange("p j (m t e) -> p m t j e", t=PACK, e=2)[:, :, t0:t1])

        def quantize_val(a, t0, t1):
            nc.vector.quantize_mx(out=val_codes[a][:, P * t0:P * t1].bitcast(FP8X4), scales=val_scales[a][:, P * t0:P * t1],
                                  in_=val_bf[a][:, t0:t1].rearrange("p t m j -> p (t m j)"))

        sig = [keep.tile([P, PACK, HALF], F32, name="sig%d" % h, tag="sig%d" % h, align_bytes=64) for h in range(2)]
        squashed = [keep.tile([P, PACK, HALF], F32, name="squashed%d" % h) for h in range(2)]
        baseline = [keep.tile([P, PACK, HALF], F32, name="baseline0", tag="val_bf1", align_bytes=64),
                    keep.tile([P, PACK, HALF], F32, name="baseline1")]
        gated = [keep.tile([P, PACK, HALF], F32, name="gated%d" % h, tag="gated%d" % h, align_bytes=64) for h in range(2)]

        gate_acc = {(half, t): bank(PACK * half + t) for half in range(2) for t in range(PACK)}
        for half in range(2):
            gather(0, half)
            for t in range(PACK):
                gate_pass(gate_acc[half, t], 0, t, half)
        for half in range(2):
            gather(1, half)
            for t in range(PACK):
                gate_pass(gate_acc[half, t], 1, t, half)
        nc.vector.tensor_copy(base_codes[:].rearrange("p a (t m e) -> p a t m e", t=PACK, e=2),
                              base_raw[:].rearrange("p (a m t e) -> p a t m e", a=PASSES, t=PACK, e=2))

        wq_raw = reuse.tile([P, PACK, N], F32, name="wq_raw", align_bytes=64, offset=BASE_AT)
        for e in range(2):
            nc.sync.dma_start(wq_raw[e:P:2], wq.rearrange("(m t e) n -> e m t n", t=PACK, e=2)[e])

        def sigmoids(half, slices):
            for t in slices:
                nc.scalar.activation(sig[half][:, t, :], gate_acc[half, t][:], ACT.Sigmoid)

        base_acc = {}

        def bases(half, slices, first_bank):
            for t in slices:
                base_acc[half, t] = bank(first_bank + t)
                for a in range(PASSES):
                    base_pass(base_acc[half, t], a, t, half)

        def tanhs(half, slices):
            for t in slices:
                nc.scalar.activation(squashed[half][:, t, :], base_acc[half, t][:], ACT.Tanh)

        def scale_baseline(half, slices):
            for t in slices:
                nc.gpsimd.tensor_scalar(baseline[half][:, t, :], squashed[half][:, t, :], gains[:, 2 * t:2 * t + 1], 0.0,
                                        ALU.mult, ALU.add)

        def scale_baseline_part(half, slices, lo, width):
            for t in slices:
                nc.scalar.activation(baseline[half][:, t, lo:lo + width], squashed[half][:, t, lo:lo + width],
                                     ACT.Copy, scale=gains[:, 2 * t:2 * t + 1])

        def values(half, slices, first_bank=0):
            for t in slices:
                acc = bank(first_bank + t)
                first = 0 if (half, t) == (0, 0) else 1
                for a in (first, 1 - first):
                    val_pass(acc, a, t, half, first)
                nc.vector.tensor_tensor(gated[half][:, t, :], acc[:], sig[half][:, t, :], ALU.mult)

        chunks = [(0, 512), (512, 128), (640, 128), (768, 128), (896, 128)]
        h_mixed = [keep.tile([P, width, PACK], BF16, name="h_mixed%d" % i, align_bytes=64)
                   for i, (c0, width) in enumerate(chunks)]
        h_codes = [keep.tile([P, width], U32, name="h_codes%d" % i, align_bytes=64) for i, (c0, width) in enumerate(chunks)]
        h_scales = [keep.tile([P, width], U8, name="h_scales%d" % i, align_bytes=64) for i, (c0, width) in enumerate(chunks)]

        def subtract(i, width):
            half, lo = divmod(chunks[i][0], HALF)
            nc.vector.tensor_tensor(h_mixed[i][:, 0:width].rearrange("p (c e) t -> p c t e", e=2),
                                    gated[half][:, :, lo:lo + width].rearrange("p t (c e) -> p c t e", e=2),
                                    baseline[half][:, :, lo:lo + width].rearrange("p t (c e) -> p c t e", e=2),
                                    ALU.subtract)

        def quantize_h(i):
            nc.vector.quantize_mx(out=h_codes[i][:].bitcast(FP8X4), scales=h_scales[i][:],
                                  in_=h_mixed[i][:].rearrange("p c t -> p (c t)"))

        wq_bf = keep.tile([P, N, PACK], BF16, name="wq_bf", align_bytes=64)
        wq_codes = keep.tile([P, N], U32, name="wq_codes", align_bytes=64)
        wq_scales = keep.tile([P, N], U8, name="wq_scales", align_bytes=64)

        pair = keep.tile([P, N // P, 256], F32, name="pair")

        def finish(i, banks, copies):
            c0, width = chunks[i]
            if i not in (1, 2):
                result = keep.tile([P, N // P, width], F32, name="result%d" % i)
            else:
                result = pair[:, :, c0 - HALF:c0 - HALF + width]
            for nt in range(N // P):
                acc = bank(banks[nt])
                nc.tensor.matmul_mx(out=acc[:, 0:width], lhsT=wq_codes[:, P * nt:P * (nt + 1)].bitcast(FP8X4),
                                    lhsT_scale=wq_scales[:, P * nt:P * (nt + 1)],
                                    rhs=h_codes[i][:].bitcast(FP8X4), rhs_scale=h_scales[i][:], start=True, stop=True)
                copies[nt](result[:, nt, :], acc[:, 0:width])
                if i == 0:
                    nc.sync.dma_start(out[P * nt:P * (nt + 1), c0:c0 + width], result[:, nt, :])
            if i > 2:
                nc.sync.dma_start(out[:, c0:c0 + width].rearrange("(u p) c -> p u c", p=P), result[:])
            if i == 2:
                nc.sync.dma_start(out[:, HALF:HALF + 256].rearrange("(u p) c -> p u c", p=P), pair[:])

        early, late = (0,), (1, 2, 3)
        sigmoids(0, range(PACK))
        bases(0, range(PACK), 0)
        sigmoids(1, early)
        bases(1, early, PACK)
        tanhs(0, range(PACK))
        cast_val(0)
        quantize_val(0, 0, PACK)
        cast_val(1)
        cast_val(2, 0, 2)
        cast_val(2, 2, PACK)
        for t in range(PACK):
            quantize_val(1, t, t + 1)
        values(0, range(PACK))
        scale_baseline(0, (0, 1, 2))
        sigmoids(1, late)
        scale_baseline_part(0, (3,), 0, HALF)
        values(1, (0,))
        values(1, (1, 2), PACK)
        tanhs(1, early)
        bases(1, late, 0)
        nc.scalar.copy(wq_bf[:].rearrange("p (c e) t -> p c t e", e=2), wq_raw[:].rearrange("p t (c e) -> p c t e", e=2))
        tanhs(1, late)
        subtract(0, HALF)
        nc.vector.quantize_mx(out=wq_codes[:].bitcast(FP8X4), scales=wq_scales[:], in_=wq_bf[:].rearrange("p n t -> p (n t)"))
        values(1, (3,), PACK)
        for lo in (0, HALF // 2):
            scale_baseline_part(1, range(PACK), lo, HALF // 2)
        quantize_h(0)
        subtract(1, 128)
        finish(0, (4, 0), (nc.scalar.copy, nc.scalar.copy))
        subtract(2, 128)
        quantize_h(1)
        finish(1, (5, 6), (nc.scalar.copy, nc.scalar.copy))
        subtract(3, 128)
        quantize_h(2)
        finish(2, (7, 1), (nc.scalar.copy, nc.scalar.copy))
        subtract(4, 128)
        quantize_h(3)
        finish(3, (2, 3), (nc.scalar.copy, nc.scalar.copy))
        quantize_h(4)
        finish(4, (4, 5), (nc.scalar.copy, nc.vector.tensor_copy))
